import numpy as np
import ml_dtypes


def mxq(x, axis, fmt="e4m3"):
    dtype, down = {"e4m3": (ml_dtypes.float8_e4m3fn, 7), "e5m2": (ml_dtypes.float8_e5m2, 14)}[fmt]
    v = np.moveaxis(np.asarray(x, np.float32).astype(ml_dtypes.bfloat16).astype(np.float64), axis, -1)
    blocks = v.reshape(v.shape[:-1] + (-1, 32))
    amax = np.abs(blocks).max(-1, keepdims=True)
    byte = np.maximum(np.where(amax > 0, np.frexp(amax)[1] - 1 + 127, 0) - down, 1)
    scale = np.exp2(byte - 127.0)
    codes = (blocks / scale).astype(np.float32).astype(dtype).astype(np.float64)
    return np.moveaxis((codes * scale).reshape(v.shape), -1, axis)


WIDE = False


def mx_kscale(k):
    if not WIDE:
        return np.ones(k)
    levels = np.array([10, -10, 5, -5, 0])
    if k % 512:
        return np.exp2(np.random.permutation(np.resize(levels, k // 32))).repeat(32)
    a = np.empty((k // 512, 16))
    for p in range(k // 512):
        a[p, :8] = np.random.permutation(np.resize(levels, 8))
        for g in range(8):
            far = levels[np.abs(levels - a[p, g]) >= 10]
            a[p, g + 8] = far[np.random.randint(len(far))]
    return np.exp2(a.ravel()).repeat(32)


def f64(x):
    return np.asarray(x).astype(np.float64)


def striped(idx):
    return np.tile(idx.reshape(-1, 16).T, (8, 1)).astype(np.uint16)


def unstriped(offs):
    return offs[:16].T.reshape(-1).astype(np.int64)


def pack_weight(w):
    k, n = w.shape
    w = f64(np.asarray(w, np.float32).astype(ml_dtypes.bfloat16)).reshape(k // 32, 32, n)
    amax = np.abs(w).max(1)
    byte = np.clip(np.where(amax > 0, np.frexp(amax)[1] - 1 + 127 - 7, 1), 1, 254)
    scaled = (w * np.exp2(127.0 - byte)[:, None, :]).reshape(k, n).astype(np.float32)
    words = np.ascontiguousarray(scaled.reshape(k // 512, 128, 4, n).transpose(0, 1, 3, 2)).astype(ml_dtypes.float8_e4m3fn).view(np.uint8)
    return words, np.ascontiguousarray(byte.astype(np.uint8).reshape(k // 512, 16, n))


def unpack_weight(words, scales):
    g, p, n, _ = words.shape
    vals = np.ascontiguousarray(words).view(ml_dtypes.float8_e4m3fn).astype(np.float64) * np.repeat(np.exp2(scales.astype(np.float64) - 127.0), 8, axis=1)[..., None]
    return vals.transpose(0, 1, 3, 2).reshape(g * 512, n)


def planes(y):
    n, m = y.shape
    v = y.astype(np.float32).astype(ml_dtypes.bfloat16).astype(np.float64).reshape(n // 32, 32, m)
    top = np.abs(v).max(1)
    byte = np.clip(np.where(top > 0, np.frexp(top)[1] - 1 + 127 - 7, 1), 1, 254)
    codes = (v * np.exp2(127.0 - byte)[:, None, :]).reshape(n, m).astype(np.float32).astype(ml_dtypes.float8_e4m3fn).view(np.uint8)
    words = codes.reshape(n // 512, 128, 4, m).transpose(0, 1, 3, 2)
    return np.ascontiguousarray(words), np.ascontiguousarray(byte.astype(np.uint8).reshape(n // 512, 16, m))


def sigmoid(v):
    return 1.0 / (1.0 + np.exp(-np.maximum(v, -700.0)))


K, T, S, W, N = 512, 2048, 512, 1024, 512


def setup_inputs():
    n = np.random.standard_normal
    s = mx_kscale(K)[:, None]
    packed_xT = pack_weight(n((K, T)) * s)
    packed_eT = pack_weight(n((K, W)) * s)
    return {
        "x_words": packed_xT[0],
        "x_scales": packed_xT[1],
        "e_words": packed_eT[0],
        "e_scales": packed_eT[1],
        "w1": (n((K, N)) / np.sqrt(2 * K) / s).astype(np.float32),
        "v1": (n((K, N)) / np.sqrt(2 * K) / s).astype(np.float32),
        "w3": (n((K, N)) / np.sqrt(2 * K) / s).astype(np.float32),
        "v3": (n((K, N)) / np.sqrt(2 * K) / s).astype(np.float32),
        "carry": (n((N, T))).astype(np.float32),
        "offs": striped(np.random.permutation(T)[:S]),
        "tok": striped(np.random.permutation(W)[:S]),
    }


def reference(x_words, x_scales, e_words, e_scales, w1, v1, w3, v3, carry, offs, tok):
    old = f64(carry)[:, unstriped(offs)]
    xq = unpack_weight(x_words, x_scales)[:, unstriped(offs)]
    e_tok = unpack_weight(e_words, e_scales)[:, unstriped(tok)]
    z = sigmoid(mxq(f64(w1), 0, "e4m3").T @ xq + mxq(f64(v1), 0, "e4m3").T @ e_tok)
    g = np.tanh(mxq(f64(w3), 0, "e4m3").T @ xq + mxq(f64(v3), 0, "e4m3").T @ e_tok)
    out_0 = old + z * (g - old)
    return (out_0,) + planes(out_0)

@@ -1,0 +1,167 @@
+from contextlib import ExitStack
+
+import concourse.mybir as mybir
+
+K, T, S, W, N = 512, 2048, 512, 1024, 512
+FLOPS = 4 * 2 * K * N * S
+
+F32 = mybir.dt.float32
+BF16 = mybir.dt.bfloat16
+I32 = mybir.dt.int32
+U32 = mybir.dt.uint32
+U16 = mybir.dt.uint16
+U8 = mybir.dt.uint8
+FP8X4 = mybir.dt.float8_e4m3fn_x4
+ALU = mybir.AluOpType
+ACT = mybir.ActivationFunctionType
+
+P = 128
+PACK = 4
+HALF = S // 2
+E_ROW = 4
+
+
+def tile_picked_zgru_mgu_po_kernel(tc, x_words, x_scales, e_words, e_scales, w1, v1, w3, v3, carry, offs, tok, out_0, out_1, out_2):
+    nc = tc.nc
+    with ExitStack() as ctx:
+        sb = ctx.enter_context(tc.tile_pool(name="sb", bufs=1))
+        ps = ctx.enter_context(tc.psum_pool(name="ps", bufs=1))
+
+        offs_t = sb.tile([P, S // 16], U16, name="offs_t")
+        tok_t = sb.tile([P, S // 16], U16, name="tok_t")
+        x_win = sb.tile([P, T], I32, name="x_win", align_bytes=64)
+        e_win = sb.tile([P, W], I32, name="e_win", align_bytes=64)
+        xs_win = sb.tile([P, T], U8, name="xs_win", align_bytes=64)
+        es_win = sb.tile([P, W], U8, name="es_win", align_bytes=64)
+        raw = {n: sb.tile([P, PACK, N], F32, name="raw_" + n, align_bytes=64) for n in ("w1", "w3", "v1", "v3")}
+        carry_win = [sb.tile([P, T], F32, name=f"carry_win{t}", align_bytes=64) for t in range(PACK)]
+        warm_in = sb.tile([P, 2], F32, name="warm_in")
+        warm_out = sb.tile([P, 2], F32, name="warm_out")
+
+        nc.vector.memset(warm_in[:], 0.0)
+        nc.scalar.activation(warm_out[:], warm_in[:], ACT.Sigmoid)
+        nc.vector.memset(xs_win[:].bitcast(I32), 0)
+        nc.vector.memset(es_win[:].bitcast(I32), 0)
+
+        def load_weight(n, src):
+            nc.sync.dma_start(out=raw[n][:], in_=src.rearrange("(p j) c -> p j c", j=PACK))
+
+        def load_words(win, src):
+            nc.sync.dma_start(out=win[:], in_=src[0].rearrange("p c r -> p (c r)").bitcast(I32))
+
+        def load_scale_rows(win, src, row):
+            for q in range(4):
+                nc.sync.dma_start(out=win[32 * q + row : 32 * q + row + 4, :].bitcast(I32), in_=src[0, 4 * q : 4 * q + 4, :].bitcast(I32))
+
+        load_weight("w1", w1)
+        load_words(x_win, x_words)
+        nc.sync.dma_start(offs_t[:], offs)
+        nc.sync.dma_start(tok_t[:], tok)
+        load_scale_rows(xs_win, x_scales, 0)
+        load_weight("w3", w3)
+        load_weight("v1", v1)
+        load_scale_rows(es_win, e_scales, E_ROW)
+        load_weight("v3", v3)
+        load_words(e_win, e_words)
+        carry_rows = carry.rearrange("(p t) c -> t p c", t=PACK)
+        for t in range(PACK):
+            nc.sync.dma_start(out=carry_win[t][:], in_=carry_rows[t])
+
+        codes = {}
+        scales = {}
+
+        def quantise_weight(n):
+            codes[n] = []
+            scales[n] = []
+            src = raw[n][:].rearrange("p j (m t) -> p m j t", t=PACK)
+            dealt = []
+            for u in range(2):
+                d = sb.tile([P, 2 * P * PACK], BF16, name=f"dealt_{n}{u}", align_bytes=64)
+                dst = d[:].rearrange("p (t m j) -> p m j t", t=2, j=PACK)
+                if u == 0:
+                    nc.vector.tensor_copy(out=dst, in_=src[:, :, :, 0:2])
+                else:
+                    nc.scalar.copy(out=dst, in_=src[:, :, :, 2:4])
+                dealt.append(d)
+            for u in range(2):
+                c = sb.tile([P, 2 * P], U32, name=f"codes_{n}{u}", align_bytes=64)
+                s = sb.tile([P, 2 * P], U8, name=f"scales_{n}{u}", align_bytes=64)
+                nc.vector.quantize_mx(out=c[:].bitcast(FP8X4), scales=s[:], in_=dealt[u][:])
+                codes[n].append(c)
+                scales[n].append(s)
+
+        xw = sb.tile([P, S], U32, name="xw", align_bytes=64)
+        xs = sb.tile([P, S], U8, name="xs", align_bytes=64)
+        ew = sb.tile([P, S], U32, name="ew", align_bytes=64)
+        es = sb.tile([P, S], U8, name="es", align_bytes=64)
+        z_acc = [ps.tile([P, S], F32, name=f"z_acc{t}") for t in range(PACK)]
+        g_acc = [ps.tile([P, S], F32, name=f"g_acc{t}") for t in range(PACK)]
+
+        def product(acc, n, t, words, plane, first):
+            cols = slice((t % 2) * P, (t % 2 + 1) * P)
+            nc.tensor.matmul_mx(
+                out=acc[:],
+                lhsT=codes[n][t // 2][:, cols].bitcast(FP8X4),
+                lhsT_scale=scales[n][t // 2][:, cols],
+                rhs=words[:].bitcast(FP8X4),
+                rhs_scale=plane,
+                start=first,
+                stop=not first,
+            )
+
+        quantise_weight("w1")
+        nc.vector.tensor_copy(xw[:], x_win[:].bitcast(U32).indirect(offs_t[:]))
+        nc.vector.tensor_copy(xs[:], xs_win[:].indirect(offs_t[:]))
+        for t in range(PACK):
+            product(z_acc[t], "w1", t, xw, xs[:], True)
+        quantise_weight("w3")
+        for t in range(PACK):
+            product(g_acc[t], "w3", t, xw, xs[:], True)
+        nc.vector.tensor_copy(es[:], es_win[:].indirect(tok_t[:]))
+        quantise_weight("v1")
+        quantise_weight("v3")
+        nc.vector.tensor_copy(ew[:], e_win[:].bitcast(U32).indirect(tok_t[:]))
+
+        y = [sb.tile([P, PACK, HALF], F32, name=f"y{h}", align_bytes=64) for h in range(2)]
+        out_rows = out_0.rearrange("(p t) c -> p t c", t=PACK)
+        for t in range(PACK):
+            product(z_acc[t], "v1", t, ew, es[E_ROW:P, :], False)
+            product(g_acc[t], "v3", t, ew, es[E_ROW:P, :], False)
+            keep = sb.tile([P, S], F32, name=f"keep{t}", align_bytes=64)
+            cand = sb.tile([P, S], F32, name=f"cand{t}", align_bytes=64)
+            nc.scalar.activation(keep[:], z_acc[t][:], ACT.Sigmoid, scale=-1.0)
+            nc.scalar.activation(cand[:], g_acc[t][:], ACT.Tanh)
+            kept = sb.tile([P, S], F32, name=f"kept{t}", align_bytes=64)
+            neg_new = sb.tile([P, S], F32, name=f"neg_new{t}", align_bytes=64)
+            if t < PACK - 1:
+                nc.vector.tensor_tensor(kept[:], carry_win[t][:].indirect(offs_t[:]), keep[:], ALU.mult)
+                nc.vector.scalar_tensor_tensor(neg_new[:], keep[:], 1.0, cand[:], ALU.subtract, ALU.mult)
+            else:
+                nc.vector.scalar_tensor_tensor(neg_new[:], keep[:], 1.0, cand[:], ALU.subtract, ALU.mult)
+                for h in range(2):
+                    cols = slice(h * HALF, (h + 1) * HALF)
+                    nc.vector.tensor_tensor(kept[:, cols], carry_win[t][:].indirect(offs_t[:, h * 16 : (h + 1) * 16]), keep[:, cols], ALU.mult)
+            for h in range(2):
+                cols = slice(h * HALF, (h + 1) * HALF)
+                nc.vector.tensor_tensor(y[h][:, t, :], kept[:, cols], neg_new[:, cols], ALU.subtract)
+            if t == PACK - 2:
+                for h in range(2):
+                    nc.sync.dma_start(out=out_rows[:, 0 : PACK - 1, h * HALF : (h + 1) * HALF], in_=y[h][:, 0 : PACK - 1, :])
+
+        y_scales = sb.tile([P, S], U8, name="y_scales", align_bytes=64)
+        out_words = out_1[0].rearrange("p c r -> p (c r)").bitcast(I32)
+        for h in range(2):
+            cols = slice(h * HALF, (h + 1) * HALF)
+            nc.sync.dma_start(out=out_rows[:, PACK - 1, cols], in_=y[h][:, PACK - 1, :])
+            y_bf = sb.tile([P, HALF * PACK], BF16, name=f"y_bf{h}", align_bytes=64)
+            dst = y_bf[:].rearrange("p (c i t) -> p c t i", i=4, t=PACK)
+            src = y[h][:].rearrange("p t (c i) -> p c t i", i=4)
+            if h == 0:
+                nc.scalar.copy(out=dst, in_=src)
+            else:
+                nc.vector.tensor_copy(out=dst, in_=src)
+            y_codes = sb.tile([P, HALF], U32, name=f"y_codes{h}", align_bytes=64)
+            nc.vector.quantize_mx(out=y_codes[:].bitcast(FP8X4), scales=y_scales[:, cols], in_=y_bf[:])
+            nc.sync.dma_start(out=out_words[:, cols], in_=y_codes[:].bitcast(I32))
+        for q in range(4):
+            nc.scalar.dma_start(out=out_2[0, 4 * q : 4 * q + 4, :].bitcast(I32), in_=y_scales[32 * q : 32 * q + 4, :].bitcast(I32))

@@ -30,7 +30,7 @@ def tile_picked_zgru_mgu_po_kernel(tc, x_words, x_scales, e_words, e_scales, w1,
         offs_t = sb.tile([P, S // 16], U16, name="offs_t")
         tok_t = sb.tile([P, S // 16], U16, name="tok_t")
         x_win = sb.tile([P, T], I32, name="x_win", align_bytes=64)
-        e_win = sb.tile([P, W], I32, name="e_win", align_bytes=64)
+        e_win = sb.tile([P, W], I32, name="e_win", tag="late", align_bytes=64)
         xs_win = sb.tile([P, T], U8, name="xs_win", align_bytes=64)
         es_win = sb.tile([P, W], U8, name="es_win", align_bytes=64)
         raw = {n: sb.tile([P, PACK, N], F32, name="raw_" + n, align_bytes=64) for n in ("w1", "w3", "v1", "v3")}
@@ -38,10 +38,10 @@ def tile_picked_zgru_mgu_po_kernel(tc, x_words, x_scales, e_words, e_scales, w1,
         warm_in = sb.tile([P, 2], F32, name="warm_in")
         warm_out = sb.tile([P, 2], F32, name="warm_out")
 
-        nc.vector.memset(warm_in[:], 0.0)
-        nc.scalar.activation(warm_out[:], warm_in[:], ACT.Sigmoid)
         nc.vector.memset(xs_win[:].bitcast(I32), 0)
         nc.vector.memset(es_win[:].bitcast(I32), 0)
+        nc.vector.memset(warm_in[:], 0.0)
+        nc.scalar.activation(warm_out[:], warm_in[:], ACT.Sigmoid)
 
         def load_weight(n, src):
             nc.sync.dma_start(out=raw[n][:], in_=src.rearrange("(p j) c -> p j c", j=PACK))
@@ -54,15 +54,15 @@ def tile_picked_zgru_mgu_po_kernel(tc, x_words, x_scales, e_words, e_scales, w1,
                 nc.sync.dma_start(out=win[32 * q + row : 32 * q + row + 4, :].bitcast(I32), in_=src[0, 4 * q : 4 * q + 4, :].bitcast(I32))
 
         load_weight("w1", w1)
-        load_words(x_win, x_words)
         nc.sync.dma_start(offs_t[:], offs)
-        nc.sync.dma_start(tok_t[:], tok)
         load_scale_rows(xs_win, x_scales, 0)
+        load_words(x_win, x_words)
         load_weight("w3", w3)
-        load_weight("v1", v1)
+        nc.sync.dma_start(tok_t[:], tok)
         load_scale_rows(es_win, e_scales, E_ROW)
-        load_weight("v3", v3)
         load_words(e_win, e_words)
+        load_weight("v1", v1)
+        load_weight("v3", v3)
         carry_rows = carry.rearrange("(p t) c -> t p c", t=PACK)
         for t in range(PACK):
             nc.sync.dma_start(out=carry_win[t][:], in_=carry_rows[t])
@@ -70,29 +70,26 @@ def tile_picked_zgru_mgu_po_kernel(tc, x_words, x_scales, e_words, e_scales, w1,
         codes = {}
         scales = {}
 
-        def quantise_weight(n):
+        def quantise_weight(n, tag, second):
             codes[n] = []
             scales[n] = []
             src = raw[n][:].rearrange("p j (m t) -> p m j t", t=PACK)
-            dealt = []
+            dealt = sb.tile([P, 2, 2 * P * PACK], BF16, name=f"dealt_{n}", tag=tag, align_bytes=64)
             for u in range(2):
-                d = sb.tile([P, 2 * P * PACK], BF16, name=f"dealt_{n}{u}", align_bytes=64)
-                dst = d[:].rearrange("p (t m j) -> p m j t", t=2, j=PACK)
+                dst = dealt[:, u, :].rearrange("p (t m j) -> p m j t", t=2, j=PACK)
                 if u == 0:
                     nc.vector.tensor_copy(out=dst, in_=src[:, :, :, 0:2])
                 else:
-                    nc.scalar.copy(out=dst, in_=src[:, :, :, 2:4])
-                dealt.append(d)
+                    second(out=dst, in_=src[:, :, :, 2:4])
             for u in range(2):
                 c = sb.tile([P, 2 * P], U32, name=f"codes_{n}{u}", align_bytes=64)
                 s = sb.tile([P, 2 * P], U8, name=f"scales_{n}{u}", align_bytes=64)
-                nc.vector.quantize_mx(out=c[:].bitcast(FP8X4), scales=s[:], in_=dealt[u][:])
+                nc.vector.quantize_mx(out=c[:].bitcast(FP8X4), scales=s[:], in_=dealt[:, u, :])
                 codes[n].append(c)
                 scales[n].append(s)
 
         xw = sb.tile([P, S], U32, name="xw", align_bytes=64)
         xs = sb.tile([P, S], U8, name="xs", align_bytes=64)
-        ew = sb.tile([P, S], U32, name="ew", align_bytes=64)
         es = sb.tile([P, S], U8, name="es", align_bytes=64)
         z_acc = [ps.tile([P, S], F32, name=f"z_acc{t}") for t in range(PACK)]
         g_acc = [ps.tile([P, S], F32, name=f"g_acc{t}") for t in range(PACK)]
@@ -109,59 +106,70 @@ def tile_picked_zgru_mgu_po_kernel(tc, x_words, x_scales, e_words, e_scales, w1,
                 stop=not first,
             )
 
-        quantise_weight("w1")
-        nc.vector.tensor_copy(xw[:], x_win[:].bitcast(U32).indirect(offs_t[:]))
+        quantise_weight("w1", "early", nc.scalar.copy)
         nc.vector.tensor_copy(xs[:], xs_win[:].indirect(offs_t[:]))
+        nc.vector.tensor_copy(xw[:], x_win[:].bitcast(U32).indirect(offs_t[:]))
         for t in range(PACK):
             product(z_acc[t], "w1", t, xw, xs[:], True)
-        quantise_weight("w3")
+        quantise_weight("w3", "early", nc.scalar.copy)
         for t in range(PACK):
             product(g_acc[t], "w3", t, xw, xs[:], True)
         nc.vector.tensor_copy(es[:], es_win[:].indirect(tok_t[:]))
-        quantise_weight("v1")
-        quantise_weight("v3")
+        ew = sb.tile([P, S], U32, name="ew", tag="early", align_bytes=64)
         nc.vector.tensor_copy(ew[:], e_win[:].bitcast(U32).indirect(tok_t[:]))
-
-        y = [sb.tile([P, PACK, HALF], F32, name=f"y{h}", align_bytes=64) for h in range(2)]
-        out_rows = out_0.rearrange("(p t) c -> p t c", t=PACK)
+        quantise_weight("v1", "late", nc.scalar.copy)
+        keep = []
         for t in range(PACK):
             product(z_acc[t], "v1", t, ew, es[E_ROW:P, :], False)
+            keep.append(sb.tile([P, S], F32, name=f"keep{t}", align_bytes=64))
+            nc.scalar.activation(keep[t][:], z_acc[t][:], ACT.Sigmoid, scale=-1.0)
+        quantise_weight("v3", "late", nc.vector.tensor_copy)
+
+        y = sb.tile([P, PACK, S], F32, name="y", align_bytes=64)
+        out_rows = out_0.rearrange("(p t) c -> p t c", t=PACK)
+        y_bf = []
+        for h in range(2):
+            y_bf.append(sb.tile([P, HALF * PACK], BF16, name=f"y_bf{h}", align_bytes=64))
+        for t in range(PACK):
             product(g_acc[t], "v3", t, ew, es[E_ROW:P, :], False)
-            keep = sb.tile([P, S], F32, name=f"keep{t}", align_bytes=64)
             cand = sb.tile([P, S], F32, name=f"cand{t}", align_bytes=64)
-            nc.scalar.activation(keep[:], z_acc[t][:], ACT.Sigmoid, scale=-1.0)
             nc.scalar.activation(cand[:], g_acc[t][:], ACT.Tanh)
-            kept = sb.tile([P, S], F32, name=f"kept{t}", align_bytes=64)
+            kept = sb.tile([P, S], F32, name=f"kept{t}", tag="late", align_bytes=64)
             neg_new = sb.tile([P, S], F32, name=f"neg_new{t}", align_bytes=64)
             if t < PACK - 1:
-                nc.vector.tensor_tensor(kept[:], carry_win[t][:].indirect(offs_t[:]), keep[:], ALU.mult)
-                nc.vector.scalar_tensor_tensor(neg_new[:], keep[:], 1.0, cand[:], ALU.subtract, ALU.mult)
+                nc.vector.tensor_tensor(kept[:], carry_win[t][:].indirect(offs_t[:]), keep[t][:], ALU.mult)
+                nc.vector.scalar_tensor_tensor(neg_new[:], keep[t][:], 1.0, cand[:], ALU.subtract, ALU.mult)
+                nc.vector.tensor_tensor(y[:, t, :], kept[:], neg_new[:], ALU.subtract)
+                nc.sync.dma_start(out=out_rows[:, t, :], in_=y[:, t, :])
             else:
-                nc.vector.scalar_tensor_tensor(neg_new[:], keep[:], 1.0, cand[:], ALU.subtract, ALU.mult)
+                nc.vector.scalar_tensor_tensor(neg_new[:], keep[t][:], 1.0, cand[:], ALU.subtract, ALU.mult)
                 for h in range(2):
                     cols = slice(h * HALF, (h + 1) * HALF)
-                    nc.vector.tensor_tensor(kept[:, cols], carry_win[t][:].indirect(offs_t[:, h * 16 : (h + 1) * 16]), keep[:, cols], ALU.mult)
-            for h in range(2):
-                cols = slice(h * HALF, (h + 1) * HALF)
-                nc.vector.tensor_tensor(y[h][:, t, :], kept[:, cols], neg_new[:, cols], ALU.subtract)
-            if t == PACK - 2:
+                    nc.vector.tensor_tensor(kept[:, cols], carry_win[t][:].indirect(offs_t[:, h * 16 : (h + 1) * 16]), keep[t][:, cols], ALU.mult)
                 for h in range(2):
-                    nc.sync.dma_start(out=out_rows[:, 0 : PACK - 1, h * HALF : (h + 1) * HALF], in_=y[h][:, 0 : PACK - 1, :])
+                    cols = slice(h * HALF, (h + 1) * HALF)
+                    nc.vector.tensor_tensor(y[:, t, cols], kept[:, cols], neg_new[:, cols], ALU.subtract)
+            if t == 1:
+                for h in range(2):
+                    cols = slice(h * HALF, (h + 1) * HALF)
+                    nc.scalar.copy(
+                        out=y_bf[h][:].rearrange("p (c i t) -> p c t i", i=4, t=PACK)[:, :, 0:2, :],
+                        in_=y[:, 0:2, cols].rearrange("p t (c i) -> p c t i", i=4),
+                    )
 
         y_scales = sb.tile([P, S], U8, name="y_scales", align_bytes=64)
         out_words = out_1[0].rearrange("p c r -> p (c r)").bitcast(I32)
         for h in range(2):
             cols = slice(h * HALF, (h + 1) * HALF)
-            nc.sync.dma_start(out=out_rows[:, PACK - 1, cols], in_=y[h][:, PACK - 1, :])
-            y_bf = sb.tile([P, HALF * PACK], BF16, name=f"y_bf{h}", align_bytes=64)
-            dst = y_bf[:].rearrange("p (c i t) -> p c t i", i=4, t=PACK)
-            src = y[h][:].rearrange("p t (c i) -> p c t i", i=4)
+            nc.sync.dma_start(out=out_rows[:, PACK - 1, cols], in_=y[:, PACK - 1, cols])
+            dst = y_bf[h][:].rearrange("p (c i t) -> p c t i", i=4, t=PACK)[:, :, 2:4, :]
+            src = y[:, 2:4, cols].rearrange("p t (c i) -> p c t i", i=4)
             if h == 0:
                 nc.scalar.copy(out=dst, in_=src)
             else:
                 nc.vector.tensor_copy(out=dst, in_=src)
             y_codes = sb.tile([P, HALF], U32, name=f"y_codes{h}", align_bytes=64)
-            nc.vector.quantize_mx(out=y_codes[:].bitcast(FP8X4), scales=y_scales[:, cols], in_=y_bf[:])
+            nc.vector.quantize_mx(out=y_codes[:].bitcast(FP8X4), scales=y_scales[:, cols], in_=y_bf[h][:])
             nc.sync.dma_start(out=out_words[:, cols], in_=y_codes[:].bitcast(I32))
         for q in range(4):
             nc.scalar.dma_start(out=out_2[0, 4 * q : 4 * q + 4, :].bitcast(I32), in_=y_scales[32 * q : 32 * q + 4, :].bitcast(I32))

@@ -50,8 +50,9 @@ def tile_picked_zgru_mgu_po_kernel(tc, x_words, x_scales, e_words, e_scales, w1,
             nc.sync.dma_start(out=win[:], in_=src[0].rearrange("p c r -> p (c r)").bitcast(I32))
 
         def load_scale_rows(win, src, row):
-            for q in range(4):
-                nc.sync.dma_start(out=win[32 * q + row : 32 * q + row + 4, :].bitcast(I32), in_=src[0, 4 * q : 4 * q + 4, :].bitcast(I32))
+            rows = src[0].rearrange("(q r) c -> r q c", r=4)
+            for r in range(4):
+                nc.gpsimd.dma_start(out=win[row + r : P : 32, :].bitcast(I32), in_=rows[r].bitcast(I32))
 
         load_weight("w1", w1)
         nc.sync.dma_start(offs_t[:], offs)
@@ -132,9 +133,9 @@ def tile_picked_zgru_mgu_po_kernel(tc, x_words, x_scales, e_words, e_scales, w1,
             y_bf.append(sb.tile([P, HALF * PACK], BF16, name=f"y_bf{h}", align_bytes=64))
         for t in range(PACK):
             product(g_acc[t], "v3", t, ew, es[E_ROW:P, :], False)
-            cand = sb.tile([P, S], F32, name=f"cand{t}", align_bytes=64)
+            cand = sb.tile([P, S], F32, name=f"cand{t}", tag=f"cand{t}", align_bytes=64)
             nc.scalar.activation(cand[:], g_acc[t][:], ACT.Tanh)
-            kept = sb.tile([P, S], F32, name=f"kept{t}", tag="late", align_bytes=64)
+            kept = sb.tile([P, S], F32, name=f"kept{t}", tag="late" if t == 0 else f"cand{t - 1}", align_bytes=64)
             neg_new = sb.tile([P, S], F32, name=f"neg_new{t}", align_bytes=64)
             if t < PACK - 1:
                 nc.vector.tensor_tensor(kept[:], carry_win[t][:].indirect(offs_t[:]), keep[t][:], ALU.mult)

@@ -29,49 +29,58 @@ def tile_picked_zgru_mgu_po_kernel(tc, x_words, x_scales, e_words, e_scales, w1,
 
         offs_t = sb.tile([P, S // 16], U16, name="offs_t")
         tok_t = sb.tile([P, S // 16], U16, name="tok_t")
-        x_win = sb.tile([P, T], I32, name="x_win", align_bytes=64)
+        x_win = sb.tile([P, T], I32, name="x_win", tag="x_c0", align_bytes=64)
         e_win = sb.tile([P, W], I32, name="e_win", tag="late", align_bytes=64)
-        xs_win = sb.tile([P, T], U8, name="xs_win", align_bytes=64)
-        es_win = sb.tile([P, W], U8, name="es_win", align_bytes=64)
-        raw = {n: sb.tile([P, PACK, N], F32, name="raw_" + n, align_bytes=64) for n in ("w1", "w3", "v1", "v3")}
-        carry_win = [sb.tile([P, T], F32, name=f"carry_win{t}", align_bytes=64) for t in range(PACK)]
+        xs_win = sb.tile([P, T], U8, name="xs_win", tag="xs_v1_c2", align_bytes=64)
+        es_win = sb.tile([P, W], U8, name="es_win", tag="es_v3_c3", align_bytes=64)
+        raw = {}
+        carry_win = []
+        xs_plane = sb.tile([P, S], U8, name="xs_plane", align_bytes=64)
+        es_plane = sb.tile([P, S], U8, name="es_plane", align_bytes=64)
         warm_in = sb.tile([P, 2], F32, name="warm_in")
         warm_out = sb.tile([P, 2], F32, name="warm_out")
 
         nc.vector.memset(xs_win[:].bitcast(I32), 0)
         nc.vector.memset(es_win[:].bitcast(I32), 0)
         nc.vector.memset(warm_in[:], 0.0)
+        nc.vector.memset(xs_plane[:].bitcast(I32), 0)
+        nc.vector.memset(es_plane[:].bitcast(I32), 0)
         nc.scalar.activation(warm_out[:], warm_in[:], ACT.Sigmoid)
 
-        def load_weight(n, src):
+        def load_weight(n, src, tag):
+            raw[n] = sb.tile([P, PACK, N], F32, name="raw_" + n, tag=tag, align_bytes=64)
             nc.sync.dma_start(out=raw[n][:], in_=src.rearrange("(p j) c -> p j c", j=PACK))
 
         def load_words(win, src):
             nc.sync.dma_start(out=win[:], in_=src[0].rearrange("p c r -> p (c r)").bitcast(I32))
 
         def load_scale_rows(win, src, row):
-            rows = src[0].rearrange("(q r) c -> r q c", r=4)
-            for r in range(4):
-                nc.gpsimd.dma_start(out=win[row + r : P : 32, :].bitcast(I32), in_=rows[r].bitcast(I32))
+            nc.sync.dma_start(out=win[row:P:8, :].bitcast(I32), in_=src[0].bitcast(I32))
 
-        load_weight("w1", w1)
+        def place_scale_rows(plane, picked, row, queue):
+            for r in range(4):
+                queue.dma_start(out=plane[r:P:32, :].bitcast(I32), in_=picked[row + 8 * r : P : 32, :].bitcast(I32))
+
+        carry_rows = carry.rearrange("(p t) c -> t p c", t=PACK)
+
+        def load_carry(tag):
+            t = len(carry_win)
+            carry_win.append(sb.tile([P, T], F32, name=f"carry_win{t}", tag=tag, align_bytes=64))
+            nc.sync.dma_start(out=carry_win[t][:], in_=carry_rows[t])
+
+        load_weight("w1", w1, "w1")
         nc.sync.dma_start(offs_t[:], offs)
         load_scale_rows(xs_win, x_scales, 0)
-        load_words(x_win, x_words)
-        load_weight("w3", w3)
         nc.sync.dma_start(tok_t[:], tok)
         load_scale_rows(es_win, e_scales, E_ROW)
+        load_words(x_win, x_words)
+        load_weight("w3", w3, "w3_c1")
         load_words(e_win, e_words)
-        load_weight("v1", v1)
-        load_weight("v3", v3)
-        carry_rows = carry.rearrange("(p t) c -> t p c", t=PACK)
-        for t in range(PACK):
-            nc.sync.dma_start(out=carry_win[t][:], in_=carry_rows[t])
 
         codes = {}
         scales = {}
 
-        def quantise_weight(n, tag, second):
+        def quantise_weight(n, tag, first, second):
             codes[n] = []
             scales[n] = []
             src = raw[n][:].rearrange("p j (m t) -> p m j t", t=PACK)
@@ -79,7 +88,7 @@ def tile_picked_zgru_mgu_po_kernel(tc, x_words, x_scales, e_words, e_scales, w1,
             for u in range(2):
                 dst = dealt[:, u, :].rearrange("p (t m j) -> p m j t", t=2, j=PACK)
                 if u == 0:
-                    nc.vector.tensor_copy(out=dst, in_=src[:, :, :, 0:2])
+                    first(out=dst, in_=src[:, :, :, 0:2])
                 else:
                     second(out=dst, in_=src[:, :, :, 2:4])
             for u in range(2):
@@ -107,24 +116,32 @@ def tile_picked_zgru_mgu_po_kernel(tc, x_words, x_scales, e_words, e_scales, w1,
                 stop=not first,
             )
 
-        quantise_weight("w1", "early", nc.scalar.copy)
         nc.vector.tensor_copy(xs[:], xs_win[:].indirect(offs_t[:]))
-        nc.vector.tensor_copy(xw[:], x_win[:].bitcast(U32).indirect(offs_t[:]))
-        for t in range(PACK):
-            product(z_acc[t], "w1", t, xw, xs[:], True)
-        quantise_weight("w3", "early", nc.scalar.copy)
-        for t in range(PACK):
-            product(g_acc[t], "w3", t, xw, xs[:], True)
+        place_scale_rows(xs_plane, xs, 0, nc.sync)
+        load_weight("v1", v1, "xs_v1_c2")
         nc.vector.tensor_copy(es[:], es_win[:].indirect(tok_t[:]))
+        load_weight("v3", v3, "es_v3_c3")
+        place_scale_rows(es_plane, es, E_ROW, nc.sync)
+        quantise_weight("w1", "early", nc.scalar.copy, nc.scalar.copy)
+        nc.vector.tensor_copy(xw[:], x_win[:].bitcast(U32).indirect(offs_t[:]))
+        load_carry("x_c0")
+        for t in range(PACK):
+            product(z_acc[t], "w1", t, xw, xs_plane[:], True)
+        quantise_weight("w3", "early", nc.vector.tensor_copy, nc.scalar.copy)
+        load_carry("w3_c1")
+        for t in range(PACK):
+            product(g_acc[t], "w3", t, xw, xs_plane[:], True)
         ew = sb.tile([P, S], U32, name="ew", tag="early", align_bytes=64)
         nc.vector.tensor_copy(ew[:], e_win[:].bitcast(U32).indirect(tok_t[:]))
-        quantise_weight("v1", "late", nc.scalar.copy)
+        quantise_weight("v1", "late", nc.vector.tensor_copy, nc.scalar.copy)
+        load_carry("xs_v1_c2")
         keep = []
         for t in range(PACK):
-            product(z_acc[t], "v1", t, ew, es[E_ROW:P, :], False)
+            product(z_acc[t], "v1", t, ew, es_plane[:], False)
             keep.append(sb.tile([P, S], F32, name=f"keep{t}", align_bytes=64))
             nc.scalar.activation(keep[t][:], z_acc[t][:], ACT.Sigmoid, scale=-1.0)
-        quantise_weight("v3", "late", nc.vector.tensor_copy)
+        quantise_weight("v3", "late", nc.vector.tensor_copy, nc.vector.tensor_copy)
+        load_carry("es_v3_c3")
 
         y = sb.tile([P, PACK, S], F32, name="y", align_bytes=64)
         out_rows = out_0.rearrange("(p t) c -> p t c", t=PACK)
@@ -132,7 +149,7 @@ def tile_picked_zgru_mgu_po_kernel(tc, x_words, x_scales, e_words, e_scales, w1,
         for h in range(2):
             y_bf.append(sb.tile([P, HALF * PACK], BF16, name=f"y_bf{h}", align_bytes=64))
         for t in range(PACK):
-            product(g_acc[t], "v3", t, ew, es[E_ROW:P, :], False)
+            product(g_acc[t], "v3", t, ew, es_plane[:], False)
             cand = sb.tile([P, S], F32, name=f"cand{t}", tag=f"cand{t}", align_bytes=64)
             nc.scalar.activation(cand[:], g_acc[t][:], ACT.Tanh)
             kept = sb.tile([P, S], F32, name=f"kept{t}", tag="late" if t == 0 else f"cand{t - 1}", align_bytes=64)
@@ -173,4 +190,4 @@ def tile_picked_zgru_mgu_po_kernel(tc, x_words, x_scales, e_words, e_scales, w1,
             nc.vector.quantize_mx(out=y_codes[:].bitcast(FP8X4), scales=y_scales[:, cols], in_=y_bf[h][:])
             nc.sync.dma_start(out=out_words[:, cols], in_=y_codes[:].bitcast(I32))
         for q in range(4):
-            nc.scalar.dma_start(out=out_2[0, 4 * q : 4 * q + 4, :].bitcast(I32), in_=y_scales[32 * q : 32 * q + 4, :].bitcast(I32))
+            (nc.sync if q < 2 else nc.scalar).dma_start(out=out_2[0, 4 * q : 4 * q + 4, :].bitcast(I32), in_=y_scales[32 * q : 32 * q + 4, :].bitcast(I32))

@@ -17,8 +17,13 @@ ACT = mybir.ActivationFunctionType
 
 P = 128
 PACK = 4
+QUADRANT = 32
+BLOCK_ROWS = 8
+GROUP = 16
+LINE = 4
 HALF = S // 2
-E_ROW = 4
+X_FIRST_ROW = 0
+E_FIRST_ROW = 4
 
 
 def tile_picked_zgru_mgu_po_kernel(tc, x_words, x_scales, e_words, e_scales, w1, v1, w3, v3, carry, offs, tok, out_0, out_1, out_2):
@@ -27,25 +32,21 @@ def tile_picked_zgru_mgu_po_kernel(tc, x_words, x_scales, e_words, e_scales, w1,
         sb = ctx.enter_context(tc.tile_pool(name="sb", bufs=1))
         ps = ctx.enter_context(tc.psum_pool(name="ps", bufs=1))
 
-        offs_t = sb.tile([P, S // 16], U16, name="offs_t")
-        tok_t = sb.tile([P, S // 16], U16, name="tok_t")
-        x_win = sb.tile([P, T], I32, name="x_win", tag="x_c0", align_bytes=64)
-        e_win = sb.tile([P, W], I32, name="e_win", tag="late", align_bytes=64)
-        xs_win = sb.tile([P, T], U8, name="xs_win", tag="xs_v1_c2", align_bytes=64)
-        es_win = sb.tile([P, W], U8, name="es_win", tag="es_v3_c3", align_bytes=64)
+        offs_t = sb.tile([P, S // GROUP], U16, name="offs_t")
+        tok_t = sb.tile([P, S // GROUP], U16, name="tok_t")
+        x_win = sb.tile([P, T], I32, name="x_win", tag="x_carry0", align_bytes=64)
+        e_win = sb.tile([P, W], I32, name="e_win", tag="e_v1_v3_kept0", align_bytes=64)
+        xs_win = sb.tile([P, T], U8, name="xs_win", tag="xs_rawv1_carry2", align_bytes=64)
+        es_win = sb.tile([P, W], U8, name="es_win", tag="es_rawv3_carry3", align_bytes=64)
         raw = {}
         carry_win = []
         xs_plane = sb.tile([P, S], U8, name="xs_plane", align_bytes=64)
         es_plane = sb.tile([P, S], U8, name="es_plane", align_bytes=64)
-        warm_in = sb.tile([P, 2], F32, name="warm_in")
-        warm_out = sb.tile([P, 2], F32, name="warm_out")
 
         nc.vector.memset(xs_win[:].bitcast(I32), 0)
         nc.vector.memset(es_win[:].bitcast(I32), 0)
-        nc.vector.memset(warm_in[:], 0.0)
         nc.vector.memset(xs_plane[:].bitcast(I32), 0)
         nc.vector.memset(es_plane[:].bitcast(I32), 0)
-        nc.scalar.activation(warm_out[:], warm_in[:], ACT.Sigmoid)
 
         def load_weight(n, src, tag):
             raw[n] = sb.tile([P, PACK, N], F32, name="raw_" + n, tag=tag, align_bytes=64)
@@ -54,12 +55,15 @@ def tile_picked_zgru_mgu_po_kernel(tc, x_words, x_scales, e_words, e_scales, w1,
         def load_words(win, src):
             nc.sync.dma_start(out=win[:], in_=src[0].rearrange("p c r -> p (c r)").bitcast(I32))
 
-        def load_scale_rows(win, src, row):
-            nc.sync.dma_start(out=win[row:P:8, :].bitcast(I32), in_=src[0].bitcast(I32))
+        def load_scale_rows(win, src, first_row):
+            nc.sync.dma_start(out=win[first_row:P:BLOCK_ROWS, :].bitcast(I32), in_=src[0].bitcast(I32))
 
-        def place_scale_rows(plane, picked, row, queue):
+        def place_scale_rows(plane, picked, first_row):
             for r in range(4):
-                queue.dma_start(out=plane[r:P:32, :].bitcast(I32), in_=picked[row + 8 * r : P : 32, :].bitcast(I32))
+                nc.sync.dma_start(
+                    out=plane[r:P:QUADRANT, :].bitcast(I32),
+                    in_=picked[first_row + BLOCK_ROWS * r : P : QUADRANT, :].bitcast(I32),
+                )
 
         carry_rows = carry.rearrange("(p t) c -> t p c", t=PACK)
 
@@ -68,29 +72,25 @@ def tile_picked_zgru_mgu_po_kernel(tc, x_words, x_scales, e_words, e_scales, w1,
             carry_win.append(sb.tile([P, T], F32, name=f"carry_win{t}", tag=tag, align_bytes=64))
             nc.sync.dma_start(out=carry_win[t][:], in_=carry_rows[t])
 
-        load_weight("w1", w1, "w1")
+        load_weight("w1", w1, "raww1")
         nc.sync.dma_start(offs_t[:], offs)
-        load_scale_rows(xs_win, x_scales, 0)
+        load_scale_rows(xs_win, x_scales, X_FIRST_ROW)
         nc.sync.dma_start(tok_t[:], tok)
-        load_scale_rows(es_win, e_scales, E_ROW)
+        load_scale_rows(es_win, e_scales, E_FIRST_ROW)
         load_words(x_win, x_words)
-        load_weight("w3", w3, "w3_c1")
+        load_weight("w3", w3, "raww3_carry1")
         load_words(e_win, e_words)
 
         codes = {}
         scales = {}
 
-        def quantise_weight(n, tag, first, second):
+        def quantise_weight(n, tag, first_copy, second_copy):
             codes[n] = []
             scales[n] = []
             src = raw[n][:].rearrange("p j (m t) -> p m j t", t=PACK)
             dealt = sb.tile([P, 2, 2 * P * PACK], BF16, name=f"dealt_{n}", tag=tag, align_bytes=64)
-            for u in range(2):
-                dst = dealt[:, u, :].rearrange("p (t m j) -> p m j t", t=2, j=PACK)
-                if u == 0:
-                    first(out=dst, in_=src[:, :, :, 0:2])
-                else:
-                    second(out=dst, in_=src[:, :, :, 2:4])
+            for u, copy in enumerate((first_copy, second_copy)):
+                copy(out=dealt[:, u, :].rearrange("p (t m j) -> p m j t", t=2, j=PACK), in_=src[:, :, :, 2 * u : 2 * u + 2])
             for u in range(2):
                 c = sb.tile([P, 2 * P], U32, name=f"codes_{n}{u}", align_bytes=64)
                 s = sb.tile([P, 2 * P], U8, name=f"scales_{n}{u}", align_bytes=64)
@@ -111,48 +111,57 @@ def tile_picked_zgru_mgu_po_kernel(tc, x_words, x_scales, e_words, e_scales, w1,
                 lhsT=codes[n][t // 2][:, cols].bitcast(FP8X4),
                 lhsT_scale=scales[n][t // 2][:, cols],
                 rhs=words[:].bitcast(FP8X4),
-                rhs_scale=plane,
+                rhs_scale=plane[:],
                 start=first,
                 stop=not first,
             )
 
         nc.vector.tensor_copy(xs[:], xs_win[:].indirect(offs_t[:]))
-        place_scale_rows(xs_plane, xs, 0, nc.sync)
-        load_weight("v1", v1, "xs_v1_c2")
+        place_scale_rows(xs_plane, xs, X_FIRST_ROW)
+        load_weight("v1", v1, "xs_rawv1_carry2")
         nc.vector.tensor_copy(es[:], es_win[:].indirect(tok_t[:]))
-        load_weight("v3", v3, "es_v3_c3")
-        place_scale_rows(es_plane, es, E_ROW, nc.sync)
-        quantise_weight("w1", "early", nc.scalar.copy, nc.scalar.copy)
+        load_weight("v3", v3, "es_rawv3_carry3")
+        place_scale_rows(es_plane, es, E_FIRST_ROW)
+
+        quantise_weight("w1", "w1_w3_ew", nc.scalar.copy, nc.scalar.copy)
         nc.vector.tensor_copy(xw[:], x_win[:].bitcast(U32).indirect(offs_t[:]))
-        load_carry("x_c0")
+        load_carry("x_carry0")
         for t in range(PACK):
-            product(z_acc[t], "w1", t, xw, xs_plane[:], True)
-        quantise_weight("w3", "early", nc.vector.tensor_copy, nc.scalar.copy)
-        load_carry("w3_c1")
+            product(z_acc[t], "w1", t, xw, xs_plane, True)
+        quantise_weight("w3", "w1_w3_ew", nc.vector.tensor_copy, nc.scalar.copy)
+        load_carry("raww3_carry1")
         for t in range(PACK):
-            product(g_acc[t], "w3", t, xw, xs_plane[:], True)
-        ew = sb.tile([P, S], U32, name="ew", tag="early", align_bytes=64)
+            product(g_acc[t], "w3", t, xw, xs_plane, True)
+        ew = sb.tile([P, S], U32, name="ew", tag="w1_w3_ew", align_bytes=64)
         nc.vector.tensor_copy(ew[:], e_win[:].bitcast(U32).indirect(tok_t[:]))
-        quantise_weight("v1", "late", nc.vector.tensor_copy, nc.scalar.copy)
-        load_carry("xs_v1_c2")
+        quantise_weight("v1", "e_v1_v3_kept0", nc.vector.tensor_copy, nc.scalar.copy)
+        load_carry("xs_rawv1_carry2")
         keep = []
         for t in range(PACK):
-            product(z_acc[t], "v1", t, ew, es_plane[:], False)
+            product(z_acc[t], "v1", t, ew, es_plane, False)
             keep.append(sb.tile([P, S], F32, name=f"keep{t}", align_bytes=64))
             nc.scalar.activation(keep[t][:], z_acc[t][:], ACT.Sigmoid, scale=-1.0)
-        quantise_weight("v3", "late", nc.vector.tensor_copy, nc.vector.tensor_copy)
-        load_carry("es_v3_c3")
+        quantise_weight("v3", "e_v1_v3_kept0", nc.vector.tensor_copy, nc.vector.tensor_copy)
+        load_carry("es_rawv3_carry3")
 
         y = sb.tile([P, PACK, S], F32, name="y", align_bytes=64)
         out_rows = out_0.rearrange("(p t) c -> p t c", t=PACK)
+        halves = [slice(h * HALF, (h + 1) * HALF) for h in range(2)]
         y_bf = []
         for h in range(2):
             y_bf.append(sb.tile([P, HALF * PACK], BF16, name=f"y_bf{h}", align_bytes=64))
+
+        def round_pair(copy, h, t0):
+            copy(
+                out=y_bf[h][:].rearrange("p (c i t) -> p c t i", i=LINE, t=PACK)[:, :, t0 : t0 + 2, :],
+                in_=y[:, t0 : t0 + 2, halves[h]].rearrange("p t (c i) -> p c t i", i=LINE),
+            )
+
         for t in range(PACK):
-            product(g_acc[t], "v3", t, ew, es_plane[:], False)
-            cand = sb.tile([P, S], F32, name=f"cand{t}", tag=f"cand{t}", align_bytes=64)
+            product(g_acc[t], "v3", t, ew, es_plane, False)
+            cand = sb.tile([P, S], F32, name=f"cand{t}", tag=f"cand{t}_kept{t + 1}", align_bytes=64)
             nc.scalar.activation(cand[:], g_acc[t][:], ACT.Tanh)
-            kept = sb.tile([P, S], F32, name=f"kept{t}", tag="late" if t == 0 else f"cand{t - 1}", align_bytes=64)
+            kept = sb.tile([P, S], F32, name=f"kept{t}", tag="e_v1_v3_kept0" if t == 0 else f"cand{t - 1}_kept{t}", align_bytes=64)
             neg_new = sb.tile([P, S], F32, name=f"neg_new{t}", align_bytes=64)
             if t < PACK - 1:
                 nc.vector.tensor_tensor(kept[:], carry_win[t][:].indirect(offs_t[:]), keep[t][:], ALU.mult)
@@ -161,33 +170,26 @@ def tile_picked_zgru_mgu_po_kernel(tc, x_words, x_scales, e_words, e_scales, w1,
                 nc.sync.dma_start(out=out_rows[:, t, :], in_=y[:, t, :])
             else:
                 nc.vector.scalar_tensor_tensor(neg_new[:], keep[t][:], 1.0, cand[:], ALU.subtract, ALU.mult)
-                for h in range(2):
-                    cols = slice(h * HALF, (h + 1) * HALF)
-                    nc.vector.tensor_tensor(kept[:, cols], carry_win[t][:].indirect(offs_t[:, h * 16 : (h + 1) * 16]), keep[t][:, cols], ALU.mult)
-                for h in range(2):
-                    cols = slice(h * HALF, (h + 1) * HALF)
+                for h, cols in enumerate(halves):
+                    half_offs = offs_t[:, h * HALF // GROUP : (h + 1) * HALF // GROUP]
+                    nc.vector.tensor_tensor(kept[:, cols], carry_win[t][:].indirect(half_offs), keep[t][:, cols], ALU.mult)
+                for cols in halves:
                     nc.vector.tensor_tensor(y[:, t, cols], kept[:, cols], neg_new[:, cols], ALU.subtract)
             if t == 1:
                 for h in range(2):
-                    cols = slice(h * HALF, (h + 1) * HALF)
-                    nc.scalar.copy(
-                        out=y_bf[h][:].rearrange("p (c i t) -> p c t i", i=4, t=PACK)[:, :, 0:2, :],
-                        in_=y[:, 0:2, cols].rearrange("p t (c i) -> p c t i", i=4),
-                    )
+                    round_pair(nc.scalar.copy, h, 0)
 
         y_scales = sb.tile([P, S], U8, name="y_scales", align_bytes=64)
         out_words = out_1[0].rearrange("p c r -> p (c r)").bitcast(I32)
-        for h in range(2):
-            cols = slice(h * HALF, (h + 1) * HALF)
+        for h, copy in enumerate((nc.scalar.copy, nc.vector.tensor_copy)):
+            cols = halves[h]
             nc.sync.dma_start(out=out_rows[:, PACK - 1, cols], in_=y[:, PACK - 1, cols])
-            dst = y_bf[h][:].rearrange("p (c i t) -> p c t i", i=4, t=PACK)[:, :, 2:4, :]
-            src = y[:, 2:4, cols].rearrange("p t (c i) -> p c t i", i=4)
-            if h == 0:
-                nc.scalar.copy(out=dst, in_=src)
-            else:
-                nc.vector.tensor_copy(out=dst, in_=src)
+            round_pair(copy, h, 2)
             y_codes = sb.tile([P, HALF], U32, name=f"y_codes{h}", align_bytes=64)
             nc.vector.quantize_mx(out=y_codes[:].bitcast(FP8X4), scales=y_scales[:, cols], in_=y_bf[h][:])
             nc.sync.dma_start(out=out_words[:, cols], in_=y_codes[:].bitcast(I32))
-        for q in range(4):
-            (nc.sync if q < 2 else nc.scalar).dma_start(out=out_2[0, 4 * q : 4 * q + 4, :].bitcast(I32), in_=y_scales[32 * q : 32 * q + 4, :].bitcast(I32))
+        for q, queue in enumerate((nc.sync, nc.sync, nc.scalar, nc.scalar)):
+            queue.dma_start(
+                out=out_2[0, 4 * q : 4 * q + 4, :].bitcast(I32),
+                in_=y_scales[QUADRANT * q : QUADRANT * q + 4, :].bitcast(I32),
+            )

@@ -22,8 +22,6 @@ BLOCK_ROWS = 8
 GROUP = 16
 LINE = 4
 HALF = S // 2
-X_FIRST_ROW = 0
-E_FIRST_ROW = 4
 
 
 def tile_picked_zgru_mgu_po_kernel(tc, x_words, x_scales, e_words, e_scales, w1, v1, w3, v3, carry, offs, tok, out_0, out_1, out_2):
@@ -34,19 +32,20 @@ def tile_picked_zgru_mgu_po_kernel(tc, x_words, x_scales, e_words, e_scales, w1,
 
         offs_t = sb.tile([P, S // GROUP], U16, name="offs_t")
         tok_t = sb.tile([P, S // GROUP], U16, name="tok_t")
-        x_win = sb.tile([P, T], I32, name="x_win", tag="x_carry0", align_bytes=64)
-        e_win = sb.tile([P, W], I32, name="e_win", tag="e_v1_v3_kept0", align_bytes=64)
-        xs_win = sb.tile([P, T], U8, name="xs_win", tag="xs_rawv1_carry2", align_bytes=64)
-        es_win = sb.tile([P, W], U8, name="es_win", tag="es_rawv3_carry3", align_bytes=64)
+        x_win = sb.tile([P, T], I32, name="x_win", align_bytes=64)
+        e_win = sb.tile([P, W], I32, name="e_win", tag="e_carry0", align_bytes=64)
+        xs_win = sb.tile([P, T], U8, name="xs_win", align_bytes=64)
+        es_win = sb.tile([P, W], U8, name="es_win", tag="es_raww3_carry2", align_bytes=64)
         raw = {}
         carry_win = []
-        xs_plane = sb.tile([P, S], U8, name="xs_plane", align_bytes=64)
-        es_plane = sb.tile([P, S], U8, name="es_plane", align_bytes=64)
+        planes = sb.tile([P, 2 * S], U8, name="planes", align_bytes=64)
+        picked = sb.tile([P, 2 * S], U8, name="picked", align_bytes=64)
+        x_cols = slice(0, S)
+        e_cols = slice(S, 2 * S)
 
         nc.vector.memset(xs_win[:].bitcast(I32), 0)
         nc.vector.memset(es_win[:].bitcast(I32), 0)
-        nc.vector.memset(xs_plane[:].bitcast(I32), 0)
-        nc.vector.memset(es_plane[:].bitcast(I32), 0)
+        nc.vector.memset(planes[:].bitcast(I32), 0)
 
         def load_weight(n, src, tag):
             raw[n] = sb.tile([P, PACK, N], F32, name="raw_" + n, tag=tag, align_bytes=64)
@@ -55,15 +54,8 @@ def tile_picked_zgru_mgu_po_kernel(tc, x_words, x_scales, e_words, e_scales, w1,
         def load_words(win, src):
             nc.sync.dma_start(out=win[:], in_=src[0].rearrange("p c r -> p (c r)").bitcast(I32))
 
-        def load_scale_rows(win, src, first_row):
-            nc.sync.dma_start(out=win[first_row:P:BLOCK_ROWS, :].bitcast(I32), in_=src[0].bitcast(I32))
-
-        def place_scale_rows(plane, picked, first_row):
-            for r in range(4):
-                nc.sync.dma_start(
-                    out=plane[r:P:QUADRANT, :].bitcast(I32),
-                    in_=picked[first_row + BLOCK_ROWS * r : P : QUADRANT, :].bitcast(I32),
-                )
+        def load_scale_rows(win, src):
+            nc.sync.dma_start(out=win[0:P:BLOCK_ROWS, :].bitcast(I32), in_=src[0].bitcast(I32))
 
         carry_rows = carry.rearrange("(p t) c -> t p c", t=PACK)
 
@@ -72,77 +64,79 @@ def tile_picked_zgru_mgu_po_kernel(tc, x_words, x_scales, e_words, e_scales, w1,
             carry_win.append(sb.tile([P, T], F32, name=f"carry_win{t}", tag=tag, align_bytes=64))
             nc.sync.dma_start(out=carry_win[t][:], in_=carry_rows[t])
 
-        load_weight("w1", w1, "raww1")
+        load_weight("w1", w1, "raww1_rawv3_carry3")
         nc.sync.dma_start(offs_t[:], offs)
-        load_scale_rows(xs_win, x_scales, X_FIRST_ROW)
+        load_scale_rows(xs_win, x_scales)
         nc.sync.dma_start(tok_t[:], tok)
-        load_scale_rows(es_win, e_scales, E_FIRST_ROW)
+        load_scale_rows(es_win, e_scales)
         load_words(x_win, x_words)
-        load_weight("w3", w3, "raww3_carry1")
         load_words(e_win, e_words)
+        load_weight("v1", v1, "rawv1_carry1")
 
         codes = {}
         scales = {}
 
-        def quantise_weight(n, tag, first_copy, second_copy):
+        def quantise_weight(n, first_copy, second_copy):
             codes[n] = []
             scales[n] = []
             src = raw[n][:].rearrange("p j (m t) -> p m j t", t=PACK)
-            dealt = sb.tile([P, 2, 2 * P * PACK], BF16, name=f"dealt_{n}", tag=tag, align_bytes=64)
+            dealt = []
             for u, copy in enumerate((first_copy, second_copy)):
-                copy(out=dealt[:, u, :].rearrange("p (t m j) -> p m j t", t=2, j=PACK), in_=src[:, :, :, 2 * u : 2 * u + 2])
+                dealt.append(sb.tile([P, 2 * P * PACK], BF16, name=f"dealt_{n}{u}", align_bytes=64))
+                copy(out=dealt[u][:].rearrange("p (t m j) -> p m j t", t=2, j=PACK), in_=src[:, :, :, 2 * u : 2 * u + 2])
             for u in range(2):
                 c = sb.tile([P, 2 * P], U32, name=f"codes_{n}{u}", align_bytes=64)
                 s = sb.tile([P, 2 * P], U8, name=f"scales_{n}{u}", align_bytes=64)
-                nc.vector.quantize_mx(out=c[:].bitcast(FP8X4), scales=s[:], in_=dealt[:, u, :])
+                nc.vector.quantize_mx(out=c[:].bitcast(FP8X4), scales=s[:], in_=dealt[u][:])
                 codes[n].append(c)
                 scales[n].append(s)
 
         xw = sb.tile([P, S], U32, name="xw", align_bytes=64)
-        xs = sb.tile([P, S], U8, name="xs", align_bytes=64)
-        es = sb.tile([P, S], U8, name="es", align_bytes=64)
+        ew = sb.tile([P, S], U32, name="ew", align_bytes=64)
         z_acc = [ps.tile([P, S], F32, name=f"z_acc{t}") for t in range(PACK)]
         g_acc = [ps.tile([P, S], F32, name=f"g_acc{t}") for t in range(PACK)]
 
-        def product(acc, n, t, words, plane, first):
+        def product(acc, n, t, words, plane_cols, first):
             cols = slice((t % 2) * P, (t % 2 + 1) * P)
             nc.tensor.matmul_mx(
                 out=acc[:],
                 lhsT=codes[n][t // 2][:, cols].bitcast(FP8X4),
                 lhsT_scale=scales[n][t // 2][:, cols],
                 rhs=words[:].bitcast(FP8X4),
-                rhs_scale=plane[:],
+                rhs_scale=planes[:, plane_cols],
                 start=first,
                 stop=not first,
             )
 
-        nc.vector.tensor_copy(xs[:], xs_win[:].indirect(offs_t[:]))
-        place_scale_rows(xs_plane, xs, X_FIRST_ROW)
-        load_weight("v1", v1, "xs_rawv1_carry2")
-        nc.vector.tensor_copy(es[:], es_win[:].indirect(tok_t[:]))
-        load_weight("v3", v3, "es_rawv3_carry3")
-        place_scale_rows(es_plane, es, E_FIRST_ROW)
+        nc.vector.tensor_copy(picked[:, x_cols], xs_win[:].indirect(offs_t[:]))
+        nc.vector.tensor_copy(picked[:, e_cols], es_win[:].indirect(tok_t[:]))
+        for r in range(4):
+            nc.sync.dma_start(
+                out=planes[r:P:QUADRANT, :].bitcast(I32),
+                in_=picked[BLOCK_ROWS * r : P : QUADRANT, :].bitcast(I32),
+            )
+        load_weight("w3", w3, "es_raww3_carry2")
 
-        quantise_weight("w1", "w1_w3_ew", nc.scalar.copy, nc.scalar.copy)
+        quantise_weight("w1", nc.scalar.copy, nc.scalar.copy)
+        load_weight("v3", v3, "raww1_rawv3_carry3")
         nc.vector.tensor_copy(xw[:], x_win[:].bitcast(U32).indirect(offs_t[:]))
-        load_carry("x_carry0")
-        for t in range(PACK):
-            product(z_acc[t], "w1", t, xw, xs_plane, True)
-        quantise_weight("w3", "w1_w3_ew", nc.vector.tensor_copy, nc.scalar.copy)
-        load_carry("raww3_carry1")
-        for t in range(PACK):
-            product(g_acc[t], "w3", t, xw, xs_plane, True)
-        ew = sb.tile([P, S], U32, name="ew", tag="w1_w3_ew", align_bytes=64)
         nc.vector.tensor_copy(ew[:], e_win[:].bitcast(U32).indirect(tok_t[:]))
-        quantise_weight("v1", "e_v1_v3_kept0", nc.vector.tensor_copy, nc.scalar.copy)
-        load_carry("xs_rawv1_carry2")
+        load_carry("e_carry0")
+        for t in range(PACK):
+            product(z_acc[t], "w1", t, xw, x_cols, True)
+        quantise_weight("v1", nc.vector.tensor_copy, nc.vector.tensor_copy)
+        load_carry("rawv1_carry1")
         keep = []
         for t in range(PACK):
-            product(z_acc[t], "v1", t, ew, es_plane, False)
+            product(z_acc[t], "v1", t, ew, e_cols, False)
             keep.append(sb.tile([P, S], F32, name=f"keep{t}", align_bytes=64))
             nc.scalar.activation(keep[t][:], z_acc[t][:], ACT.Sigmoid, scale=-1.0)
-        quantise_weight("v3", "e_v1_v3_kept0", nc.vector.tensor_copy, nc.vector.tensor_copy)
-        load_carry("es_rawv3_carry3")
+        quantise_weight("w3", nc.vector.tensor_copy, nc.vector.tensor_copy)
+        load_carry("es_raww3_carry2")
+        for t in range(PACK):
+            product(g_acc[t], "w3", t, xw, x_cols, True)
+        quantise_weight("v3", nc.vector.tensor_copy, nc.scalar.copy)
+        load_carry("raww1_rawv3_carry3")
 
         y = sb.tile([P, PACK, S], F32, name="y", align_bytes=64)
         out_rows = out_0.rearrange("(p t) c -> p t c", t=PACK)
@@ -157,24 +151,22 @@ def tile_picked_zgru_mgu_po_kernel(tc, x_words, x_scales, e_words, e_scales, w1,
                 in_=y[:, t0 : t0 + 2, halves[h]].rearrange("p t (c i) -> p c t i", i=LINE),
             )
 
+        neg_new = []
         for t in range(PACK):
-            product(g_acc[t], "v3", t, ew, es_plane, False)
-            cand = sb.tile([P, S], F32, name=f"cand{t}", tag=f"cand{t}_kept{t + 1}", align_bytes=64)
+            product(g_acc[t], "v3", t, ew, e_cols, False)
+            cand = sb.tile([P, S], F32, name=f"cand{t}", align_bytes=64)
             nc.scalar.activation(cand[:], g_acc[t][:], ACT.Tanh)
-            kept = sb.tile([P, S], F32, name=f"kept{t}", tag="e_v1_v3_kept0" if t == 0 else f"cand{t - 1}_kept{t}", align_bytes=64)
-            neg_new = sb.tile([P, S], F32, name=f"neg_new{t}", align_bytes=64)
+            neg_new.append(sb.tile([P, S], F32, name=f"neg_new{t}", align_bytes=64))
+            nc.vector.scalar_tensor_tensor(neg_new[t][:], keep[t][:], 1.0, cand[:], ALU.subtract, ALU.mult)
+        for t in range(PACK):
+            kept = sb.tile([P, S], F32, name=f"kept{t}", align_bytes=64)
+            for h, cols in enumerate(halves):
+                half_offs = offs_t[:, h * HALF // GROUP : (h + 1) * HALF // GROUP]
+                nc.vector.tensor_tensor(kept[:, cols], carry_win[t][:].indirect(half_offs), keep[t][:, cols], ALU.mult)
+            for cols in halves:
+                nc.vector.tensor_tensor(y[:, t, cols], kept[:, cols], neg_new[t][:, cols], ALU.subtract)
             if t < PACK - 1:
-                nc.vector.tensor_tensor(kept[:], carry_win[t][:].indirect(offs_t[:]), keep[t][:], ALU.mult)
-                nc.vector.scalar_tensor_tensor(neg_new[:], keep[t][:], 1.0, cand[:], ALU.subtract, ALU.mult)
-                nc.vector.tensor_tensor(y[:, t, :], kept[:], neg_new[:], ALU.subtract)
                 nc.sync.dma_start(out=out_rows[:, t, :], in_=y[:, t, :])
-            else:
-                nc.vector.scalar_tensor_tensor(neg_new[:], keep[t][:], 1.0, cand[:], ALU.subtract, ALU.mult)
-                for h, cols in enumerate(halves):
-                    half_offs = offs_t[:, h * HALF // GROUP : (h + 1) * HALF // GROUP]
-                    nc.vector.tensor_tensor(kept[:, cols], carry_win[t][:].indirect(half_offs), keep[t][:, cols], ALU.mult)
-                for cols in halves:
-                    nc.vector.tensor_tensor(y[:, t, cols], kept[:, cols], neg_new[:, cols], ALU.subtract)
             if t == 1:
                 for h in range(2):
                     round_pair(nc.scalar.copy, h, 0)

@@ -1,6 +1,7 @@
 from contextlib import ExitStack
 
 import concourse.mybir as mybir
+from concourse.masks import make_identity
 
 K, T, S, W, N = 512, 2048, 512, 1024, 512
 FLOPS = 4 * 2 * K * N * S
@@ -21,6 +22,9 @@ QUADRANT = 32
 BLOCK_ROWS = 8
 GROUP = 16
 LINE = 4
+TENSOR_TILES = 2
+QUARTER = S // 4
+SCALAR_COLS = 320
 HALF = S // 2
 
 
@@ -33,22 +37,19 @@ def tile_picked_zgru_mgu_po_kernel(tc, x_words, x_scales, e_words, e_scales, w1,
         offs_t = sb.tile([P, S // GROUP], U16, name="offs_t")
         tok_t = sb.tile([P, S // GROUP], U16, name="tok_t")
         x_win = sb.tile([P, T], I32, name="x_win", align_bytes=64)
-        e_win = sb.tile([P, W], I32, name="e_win", tag="e_carry0", align_bytes=64)
         xs_win = sb.tile([P, T], U8, name="xs_win", align_bytes=64)
-        es_win = sb.tile([P, W], U8, name="es_win", tag="es_raww3_carry2", align_bytes=64)
+        es_win = sb.tile([P, W], U8, name="es_win", align_bytes=64)
         raw = {}
         carry_win = []
         planes = sb.tile([P, 2 * S], U8, name="planes", align_bytes=64)
         picked = sb.tile([P, 2 * S], U8, name="picked", align_bytes=64)
-        x_cols = slice(0, S)
-        e_cols = slice(S, 2 * S)
+        plane_cols = {"x": slice(0, S), "e": slice(S, 2 * S)}
 
         nc.vector.memset(xs_win[:].bitcast(I32), 0)
-        nc.vector.memset(es_win[:].bitcast(I32), 0)
-        nc.vector.memset(planes[:].bitcast(I32), 0)
+        nc.gpsimd.memset(es_win[:].bitcast(I32), 0)
 
-        def load_weight(n, src, tag):
-            raw[n] = sb.tile([P, PACK, N], F32, name="raw_" + n, tag=tag, align_bytes=64)
+        def load_weight(n, src):
+            raw[n] = sb.tile([P, PACK, N], F32, name="raw_" + n, align_bytes=64)
             nc.sync.dma_start(out=raw[n][:], in_=src.rearrange("(p j) c -> p j c", j=PACK))
 
         def load_words(win, src):
@@ -59,127 +60,163 @@ def tile_picked_zgru_mgu_po_kernel(tc, x_words, x_scales, e_words, e_scales, w1,
 
         carry_rows = carry.rearrange("(p t) c -> t p c", t=PACK)
 
-        def load_carry(tag):
+        def load_carry():
             t = len(carry_win)
-            carry_win.append(sb.tile([P, T], F32, name=f"carry_win{t}", tag=tag, align_bytes=64))
+            carry_win.append(sb.tile([P, T], F32, name=f"carry_win{t}", align_bytes=64))
             nc.sync.dma_start(out=carry_win[t][:], in_=carry_rows[t])
 
-        load_weight("w1", w1, "raww1_rawv3_carry3")
+        load_weight("w1", w1)
         nc.sync.dma_start(offs_t[:], offs)
-        load_scale_rows(xs_win, x_scales)
         nc.sync.dma_start(tok_t[:], tok)
+        load_scale_rows(xs_win, x_scales)
         load_scale_rows(es_win, e_scales)
         load_words(x_win, x_words)
+        load_weight("w3", w3)
+        e_win = sb.tile([P, W], I32, name="e_win", align_bytes=64)
         load_words(e_win, e_words)
-        load_weight("v1", v1, "rawv1_carry1")
 
         codes = {}
         scales = {}
 
-        def quantise_weight(n, first_copy, second_copy):
-            codes[n] = []
-            scales[n] = []
+        def quantise_weight(n, copies, pieces):
             src = raw[n][:].rearrange("p j (m t) -> p m j t", t=PACK)
-            dealt = []
-            for u, copy in enumerate((first_copy, second_copy)):
-                dealt.append(sb.tile([P, 2 * P * PACK], BF16, name=f"dealt_{n}{u}", align_bytes=64))
-                copy(out=dealt[u][:].rearrange("p (t m j) -> p m j t", t=2, j=PACK), in_=src[:, :, :, 2 * u : 2 * u + 2])
+            dealt = sb.tile([P, N * PACK], BF16, name=f"dealt_{n}", align_bytes=64)
             for u in range(2):
-                c = sb.tile([P, 2 * P], U32, name=f"codes_{n}{u}", align_bytes=64)
-                s = sb.tile([P, 2 * P], U8, name=f"scales_{n}{u}", align_bytes=64)
-                nc.vector.quantize_mx(out=c[:].bitcast(FP8X4), scales=s[:], in_=dealt[u][:])
-                codes[n].append(c)
-                scales[n].append(s)
+                pair = dealt[:, u * 2 * N : (u + 1) * 2 * N].rearrange("p (t m j) -> p m j t", t=2, j=PACK)
+                copies[u](out=pair, in_=src[:, :, :, 2 * u : 2 * u + 2])
+            codes[n] = sb.tile([P, N], U32, name=f"codes_{n}", align_bytes=64)
+            scales[n] = sb.tile([P, N], U8, name=f"scales_{n}", align_bytes=64)
+            width = N // pieces
+            for u in range(pieces):
+                cols = slice(u * width, (u + 1) * width)
+                nc.vector.quantize_mx(out=codes[n][:, cols].bitcast(FP8X4), scales=scales[n][:, cols], in_=dealt[:, u * width * PACK : (u + 1) * width * PACK])
 
         xw = sb.tile([P, S], U32, name="xw", align_bytes=64)
         ew = sb.tile([P, S], U32, name="ew", align_bytes=64)
-        z_acc = [ps.tile([P, S], F32, name=f"z_acc{t}") for t in range(PACK)]
-        g_acc = [ps.tile([P, S], F32, name=f"g_acc{t}") for t in range(PACK)]
+        z_acc = [ps.tile([P, S], F32, name=f"z_acc{t}", tag=f"bank{t}") for t in range(PACK)]
+        ident = sb.tile([P, P], F32, name="ident", align_bytes=64)
+        make_identity(nc, ident[:])
+        g_acc = [ps.tile([P, S], F32, name=f"g_acc{t}", tag=f"bank{PACK + t}") for t in range(PACK)]
 
-        def product(acc, n, t, words, plane_cols, first):
-            cols = slice((t % 2) * P, (t % 2 + 1) * P)
+        def product(acc, n, t, words, table, first):
+            cols = slice(t * P, (t + 1) * P)
             nc.tensor.matmul_mx(
                 out=acc[:],
-                lhsT=codes[n][t // 2][:, cols].bitcast(FP8X4),
-                lhsT_scale=scales[n][t // 2][:, cols],
+                lhsT=codes[n][:, cols].bitcast(FP8X4),
+                lhsT_scale=scales[n][:, cols],
                 rhs=words[:].bitcast(FP8X4),
-                rhs_scale=planes[:, plane_cols],
+                rhs_scale=planes[:, plane_cols[table]],
                 start=first,
                 stop=not first,
             )
 
-        nc.vector.tensor_copy(picked[:, x_cols], xs_win[:].indirect(offs_t[:]))
-        nc.vector.tensor_copy(picked[:, e_cols], es_win[:].indirect(tok_t[:]))
-        for r in range(4):
+        nc.vector.tensor_copy(picked[:, plane_cols["x"]], xs_win[:].indirect(offs_t[:]))
+        nc.vector.tensor_copy(picked[:, plane_cols["e"]], es_win[:].indirect(tok_t[:]))
+        nc.vector.tensor_copy(planes[:].bitcast(I32), picked[:].bitcast(I32))
+        for r in range(1, 4):
             nc.sync.dma_start(
                 out=planes[r:P:QUADRANT, :].bitcast(I32),
                 in_=picked[BLOCK_ROWS * r : P : QUADRANT, :].bitcast(I32),
             )
-        load_weight("w3", w3, "es_raww3_carry2")
+        load_weight("v1", v1)
+        load_weight("v3", v3)
+        for t in range(PACK):
+            load_carry()
 
-        quantise_weight("w1", nc.scalar.copy, nc.scalar.copy)
-        load_weight("v3", v3, "raww1_rawv3_carry3")
         nc.vector.tensor_copy(xw[:], x_win[:].bitcast(U32).indirect(offs_t[:]))
+        quantise_weight("w1", (nc.scalar.copy, nc.scalar.copy), 1)
+        for t in range(PACK):
+            product(z_acc[t], "w1", t, xw, "x", True)
         nc.vector.tensor_copy(ew[:], e_win[:].bitcast(U32).indirect(tok_t[:]))
-        load_carry("e_carry0")
+        quantise_weight("w3", (nc.scalar.copy, nc.scalar.copy), 1)
         for t in range(PACK):
-            product(z_acc[t], "w1", t, xw, x_cols, True)
-        quantise_weight("v1", nc.vector.tensor_copy, nc.vector.tensor_copy)
-        load_carry("rawv1_carry1")
-        keep = []
+            product(g_acc[t], "w3", t, xw, "x", True)
+        quantise_weight("v1", (nc.vector.tensor_copy, nc.vector.tensor_copy), 2)
+        keep = sb.tile([P, PACK, S], F32, name="keep", align_bytes=64)
         for t in range(PACK):
-            product(z_acc[t], "v1", t, ew, e_cols, False)
-            keep.append(sb.tile([P, S], F32, name=f"keep{t}", align_bytes=64))
-            nc.scalar.activation(keep[t][:], z_acc[t][:], ACT.Sigmoid, scale=-1.0)
-        quantise_weight("w3", nc.vector.tensor_copy, nc.vector.tensor_copy)
-        load_carry("es_raww3_carry2")
-        for t in range(PACK):
-            product(g_acc[t], "w3", t, xw, x_cols, True)
-        quantise_weight("v3", nc.vector.tensor_copy, nc.scalar.copy)
-        load_carry("raww1_rawv3_carry3")
+            product(z_acc[t], "v1", t, ew, "e", False)
+            nc.scalar.activation(keep[:, t, :], z_acc[t][:], ACT.Sigmoid, scale=-1.0)
+        quantise_weight("v3", (nc.vector.tensor_copy, nc.vector.tensor_copy), 2)
 
         y = sb.tile([P, PACK, S], F32, name="y", align_bytes=64)
         out_rows = out_0.rearrange("(p t) c -> p t c", t=PACK)
         halves = [slice(h * HALF, (h + 1) * HALF) for h in range(2)]
-        y_bf = []
-        for h in range(2):
-            y_bf.append(sb.tile([P, HALF * PACK], BF16, name=f"y_bf{h}", align_bytes=64))
+        y_bf = sb.tile([P, S * PACK], BF16, name="y_bf", align_bytes=64)
 
-        def round_pair(copy, h, t0):
+        def round_result(copy, c0, c1):
             copy(
-                out=y_bf[h][:].rearrange("p (c i t) -> p c t i", i=LINE, t=PACK)[:, :, t0 : t0 + 2, :],
-                in_=y[:, t0 : t0 + 2, halves[h]].rearrange("p t (c i) -> p c t i", i=LINE),
+                out=y_bf[:, c0 * PACK : c1 * PACK].rearrange("p (c i t) -> p c t i", i=LINE, t=PACK),
+                in_=y[:, :, c0:c1].rearrange("p t (c i) -> p c t i", i=LINE),
             )
 
-        neg_new = []
+        cand = sb.tile([P, PACK, S], F32, name="cand", align_bytes=64)
         for t in range(PACK):
-            product(g_acc[t], "v3", t, ew, e_cols, False)
-            cand = sb.tile([P, S], F32, name=f"cand{t}", align_bytes=64)
-            nc.scalar.activation(cand[:], g_acc[t][:], ACT.Tanh)
-            neg_new.append(sb.tile([P, S], F32, name=f"neg_new{t}", align_bytes=64))
-            nc.vector.scalar_tensor_tensor(neg_new[t][:], keep[t][:], 1.0, cand[:], ALU.subtract, ALU.mult)
-        for t in range(PACK):
-            kept = sb.tile([P, S], F32, name=f"kept{t}", align_bytes=64)
-            for h, cols in enumerate(halves):
-                half_offs = offs_t[:, h * HALF // GROUP : (h + 1) * HALF // GROUP]
-                nc.vector.tensor_tensor(kept[:, cols], carry_win[t][:].indirect(half_offs), keep[t][:, cols], ALU.mult)
-            for cols in halves:
-                nc.vector.tensor_tensor(y[:, t, cols], kept[:, cols], neg_new[t][:, cols], ALU.subtract)
-            if t < PACK - 1:
-                nc.sync.dma_start(out=out_rows[:, t, :], in_=y[:, t, :])
-            if t == 1:
-                for h in range(2):
-                    round_pair(nc.scalar.copy, h, 0)
+            product(g_acc[t], "v3", t, ew, "e", False)
+            nc.scalar.activation(cand[:, t, :], g_acc[t][:], ACT.Tanh, scale=-1.0)
+
+        fresh = sb.tile([P, PACK, S], F32, name="fresh", align_bytes=64)
+        kept = sb.tile([P, PACK, S], F32, name="kept", align_bytes=64)
+        last = PACK - 1
+
+        def look_up(t, cols):
+            part_offs = offs_t[:, cols.start // GROUP : cols.stop // GROUP]
+            nc.vector.tensor_tensor(kept[:, t, cols], carry_win[t][:].indirect(part_offs), keep[:, t, cols], ALU.mult)
+
+        def add_on_vector(t, cols):
+            nc.vector.tensor_tensor(y[:, t, cols], kept[:, t, cols], fresh[:, t, cols], ALU.add)
+
+        for t in range(TENSOR_TILES):
+            look_up(t, slice(0, S))
+            pair = slice(2 * t, 2 * t + 2)
+            nc.vector.scalar_tensor_tensor(fresh[:, pair, :], keep[:, pair, :], 1.0, cand[:, pair, :], ALU.subtract, ALU.mult)
+        def add_on_tensor(t, cols, banks):
+            width = cols.stop - cols.start
+            parts = [slice(b, b + P) for b in range(0, width, P)]
+            turned_acc = ps.tile([P, width], F32, name=f"turned_acc{t}_{cols.start}", tag=f"bank{banks[0]}")
+            for i, term in enumerate((kept, fresh) if t == 0 else (fresh, kept)):
+                for b, part in enumerate(parts):
+                    nc.tensor.matmul(turned_acc[:, part], lhsT=term[:, t, cols][:, part], rhs=ident[:], is_transpose=True, start=(i == 0 and b == 0), stop=(i == 1 and b == len(parts) - 1))
+            turned = sb.tile([P, width], F32, name=f"turned{t}_{cols.start}", align_bytes=64)
+            nc.scalar.copy(out=turned[:], in_=turned_acc[:])
+            back_acc = ps.tile([P, width], F32, name=f"back_acc{t}_{cols.start}", tag=f"bank{banks[1]}")
+            for part in parts:
+                nc.tensor.transpose(back_acc[:, part], turned[:, part], ident[:])
+            nc.scalar.copy(out=y[:, t, cols], in_=back_acc[:])
+
+        add_on_tensor(0, slice(0, S), (0, 1))
+        nc.sync.dma_start(out=out_rows[:, 0, :], in_=y[:, 0, :])
+        add_on_tensor(1, halves[0], (2, 4))
+        add_on_tensor(1, halves[1], (3, 5))
+        nc.sync.dma_start(out=out_rows[:, 1, :], in_=y[:, 1, :])
+        for cols in halves:
+            look_up(2, cols)
+        for cols in halves:
+            add_on_vector(2, cols)
+        nc.sync.dma_start(out=out_rows[:, 2, :], in_=y[:, 2, :])
+        quarters = [slice(h * QUARTER, (h + 1) * QUARTER) for h in range(4)]
+        look_up(last, quarters[0])
+        for h, cols in enumerate(quarters):
+            if h + 1 < len(quarters):
+                look_up(last, quarters[h + 1])
+            add_on_vector(last, cols)
+        nc.sync.dma_start(out=out_rows[:, last, :], in_=y[:, last, :])
 
         y_scales = sb.tile([P, S], U8, name="y_scales", align_bytes=64)
+        y_codes = sb.tile([P, S], U32, name="y_codes", align_bytes=64)
         out_words = out_1[0].rearrange("p c r -> p (c r)").bitcast(I32)
-        for h, copy in enumerate((nc.scalar.copy, nc.vector.tensor_copy)):
-            cols = halves[h]
-            nc.sync.dma_start(out=out_rows[:, PACK - 1, cols], in_=y[:, PACK - 1, cols])
-            round_pair(copy, h, 2)
-            y_codes = sb.tile([P, HALF], U32, name=f"y_codes{h}", align_bytes=64)
-            nc.vector.quantize_mx(out=y_codes[:].bitcast(FP8X4), scales=y_scales[:, cols], in_=y_bf[h][:])
-            nc.sync.dma_start(out=out_words[:, cols], in_=y_codes[:].bitcast(I32))
+
+        def quantise_result(cols):
+            nc.vector.quantize_mx(out=y_codes[:, cols].bitcast(FP8X4), scales=y_scales[:, cols], in_=y_bf[:, cols.start * PACK : cols.stop * PACK])
+
+        for cols in quarters[:2]:
+            round_result(nc.scalar.copy, cols.start, cols.stop)
+        round_result(nc.scalar.copy, HALF, SCALAR_COLS)
+        quantise_result(quarters[0])
+        round_result(nc.vector.tensor_copy, SCALAR_COLS, S)
+        quantise_result(quarters[1])
+        quantise_result(halves[1])
+        for cols in halves:
+            nc.sync.dma_start(out=out_words[:, cols], in_=y_codes[:, cols].bitcast(I32))
         for q, queue in enumerate((nc.sync, nc.sync, nc.scalar, nc.scalar)):
             queue.dma_start(
                 out=out_2[0, 4 * q : 4 * q + 4, :].bitcast(I32),

@@ -1,7 +1,6 @@
 from contextlib import ExitStack
 
 import concourse.mybir as mybir
-from concourse.masks import make_identity
 
 K, T, S, W, N = 512, 2048, 512, 1024, 512
 FLOPS = 4 * 2 * K * N * S
@@ -22,9 +21,8 @@ QUADRANT = 32
 BLOCK_ROWS = 8
 GROUP = 16
 LINE = 4
-TENSOR_TILES = 2
-QUARTER = S // 4
 SCALAR_COLS = 320
+QUARTER = S // 4
 HALF = S // 2
 
 
@@ -37,6 +35,7 @@ def tile_picked_zgru_mgu_po_kernel(tc, x_words, x_scales, e_words, e_scales, w1,
         offs_t = sb.tile([P, S // GROUP], U16, name="offs_t")
         tok_t = sb.tile([P, S // GROUP], U16, name="tok_t")
         x_win = sb.tile([P, T], I32, name="x_win", align_bytes=64)
+        e_win = sb.tile([P, W], I32, name="e_win", align_bytes=64)
         xs_win = sb.tile([P, T], U8, name="xs_win", align_bytes=64)
         es_win = sb.tile([P, W], U8, name="es_win", align_bytes=64)
         raw = {}
@@ -60,20 +59,14 @@ def tile_picked_zgru_mgu_po_kernel(tc, x_words, x_scales, e_words, e_scales, w1,
 
         carry_rows = carry.rearrange("(p t) c -> t p c", t=PACK)
 
-        def load_carry():
-            t = len(carry_win)
-            carry_win.append(sb.tile([P, T], F32, name=f"carry_win{t}", align_bytes=64))
-            nc.sync.dma_start(out=carry_win[t][:], in_=carry_rows[t])
-
         load_weight("w1", w1)
         nc.sync.dma_start(offs_t[:], offs)
         nc.sync.dma_start(tok_t[:], tok)
         load_scale_rows(xs_win, x_scales)
         load_scale_rows(es_win, e_scales)
-        load_words(x_win, x_words)
-        load_weight("w3", w3)
-        e_win = sb.tile([P, W], I32, name="e_win", align_bytes=64)
+        load_weight("v1", v1)
         load_words(e_win, e_words)
+        load_words(x_win, x_words)
 
         codes = {}
         scales = {}
@@ -94,8 +87,6 @@ def tile_picked_zgru_mgu_po_kernel(tc, x_words, x_scales, e_words, e_scales, w1,
         xw = sb.tile([P, S], U32, name="xw", align_bytes=64)
         ew = sb.tile([P, S], U32, name="ew", align_bytes=64)
         z_acc = [ps.tile([P, S], F32, name=f"z_acc{t}", tag=f"bank{t}") for t in range(PACK)]
-        ident = sb.tile([P, P], F32, name="ident", align_bytes=64)
-        make_identity(nc, ident[:])
         g_acc = [ps.tile([P, S], F32, name=f"g_acc{t}", tag=f"bank{PACK + t}") for t in range(PACK)]
 
         def product(acc, n, t, words, table, first):
@@ -110,6 +101,8 @@ def tile_picked_zgru_mgu_po_kernel(tc, x_words, x_scales, e_words, e_scales, w1,
                 stop=not first,
             )
 
+        on_vector = (nc.vector.tensor_copy, nc.vector.tensor_copy)
+        on_scalar = (nc.scalar.copy, nc.scalar.copy)
         nc.vector.tensor_copy(picked[:, plane_cols["x"]], xs_win[:].indirect(offs_t[:]))
         nc.vector.tensor_copy(picked[:, plane_cols["e"]], es_win[:].indirect(tok_t[:]))
         nc.vector.tensor_copy(planes[:].bitcast(I32), picked[:].bitcast(I32))
@@ -118,29 +111,30 @@ def tile_picked_zgru_mgu_po_kernel(tc, x_words, x_scales, e_words, e_scales, w1,
                 out=planes[r:P:QUADRANT, :].bitcast(I32),
                 in_=picked[BLOCK_ROWS * r : P : QUADRANT, :].bitcast(I32),
             )
-        load_weight("v1", v1)
+        load_weight("w3", w3)
         load_weight("v3", v3)
         for t in range(PACK):
-            load_carry()
+            carry_win.append(sb.tile([P, T], F32, name=f"carry_win{t}", tag=f"carry{t}", align_bytes=64))
+            nc.sync.dma_start(out=carry_win[t][:], in_=carry_rows[t])
 
-        nc.vector.tensor_copy(xw[:], x_win[:].bitcast(U32).indirect(offs_t[:]))
-        quantise_weight("w1", (nc.scalar.copy, nc.scalar.copy), 1)
-        for t in range(PACK):
-            product(z_acc[t], "w1", t, xw, "x", True)
+        quantise_weight("w1", on_scalar, 1)
         nc.vector.tensor_copy(ew[:], e_win[:].bitcast(U32).indirect(tok_t[:]))
-        quantise_weight("w3", (nc.scalar.copy, nc.scalar.copy), 1)
+        quantise_weight("v1", on_scalar, 1)
+        nc.vector.tensor_copy(xw[:], x_win[:].bitcast(U32).indirect(offs_t[:]))
+        keep = sb.tile([P, PACK, S], F32, name="keep", align_bytes=64)
+        product(z_acc[0], "v1", 0, ew, "e", True)
+        for t in range(PACK):
+            if t + 1 < PACK:
+                product(z_acc[t + 1], "v1", t + 1, ew, "e", True)
+            product(z_acc[t], "w1", t, xw, "x", False)
+            nc.scalar.activation(keep[:, t, :], z_acc[t][:], ACT.Sigmoid, scale=-1.0)
+        quantise_weight("w3", on_vector, 1)
         for t in range(PACK):
             product(g_acc[t], "w3", t, xw, "x", True)
-        quantise_weight("v1", (nc.vector.tensor_copy, nc.vector.tensor_copy), 2)
-        keep = sb.tile([P, PACK, S], F32, name="keep", align_bytes=64)
-        for t in range(PACK):
-            product(z_acc[t], "v1", t, ew, "e", False)
-            nc.scalar.activation(keep[:, t, :], z_acc[t][:], ACT.Sigmoid, scale=-1.0)
-        quantise_weight("v3", (nc.vector.tensor_copy, nc.vector.tensor_copy), 2)
+        quantise_weight("v3", (nc.vector.tensor_copy, nc.scalar.copy), 2)
 
         y = sb.tile([P, PACK, S], F32, name="y", align_bytes=64)
         out_rows = out_0.rearrange("(p t) c -> p t c", t=PACK)
-        halves = [slice(h * HALF, (h + 1) * HALF) for h in range(2)]
         y_bf = sb.tile([P, S * PACK], BF16, name="y_bf", align_bytes=64)
 
         def round_result(copy, c0, c1):
@@ -156,50 +150,50 @@ def tile_picked_zgru_mgu_po_kernel(tc, x_words, x_scales, e_words, e_scales, w1,
 
         fresh = sb.tile([P, PACK, S], F32, name="fresh", align_bytes=64)
         kept = sb.tile([P, PACK, S], F32, name="kept", align_bytes=64)
+        old = sb.tile([P, 3, S], F32, name="old", align_bytes=64)
         last = PACK - 1
+        whole = slice(0, S)
+
+        def part_of_offs(cols):
+            return offs_t[:, cols.start // GROUP : cols.stop // GROUP]
 
         def look_up(t, cols):
-            part_offs = offs_t[:, cols.start // GROUP : cols.stop // GROUP]
-            nc.vector.tensor_tensor(kept[:, t, cols], carry_win[t][:].indirect(part_offs), keep[:, t, cols], ALU.mult)
+            nc.vector.tensor_tensor(kept[:, t, cols], carry_win[t][:].indirect(part_of_offs(cols)), keep[:, t, cols], ALU.mult)
 
-        def add_on_vector(t, cols):
+        def make_fresh(tiles):
+            nc.vector.scalar_tensor_tensor(fresh[:, tiles, :], keep[:, tiles, :], 1.0, cand[:, tiles, :], ALU.subtract, ALU.mult)
+
+        def add(t, cols):
             nc.vector.tensor_tensor(y[:, t, cols], kept[:, t, cols], fresh[:, t, cols], ALU.add)
 
-        for t in range(TENSOR_TILES):
-            look_up(t, slice(0, S))
-            pair = slice(2 * t, 2 * t + 2)
-            nc.vector.scalar_tensor_tensor(fresh[:, pair, :], keep[:, pair, :], 1.0, cand[:, pair, :], ALU.subtract, ALU.mult)
-        def add_on_tensor(t, cols, banks):
-            width = cols.stop - cols.start
-            parts = [slice(b, b + P) for b in range(0, width, P)]
-            turned_acc = ps.tile([P, width], F32, name=f"turned_acc{t}_{cols.start}", tag=f"bank{banks[0]}")
-            for i, term in enumerate((kept, fresh) if t == 0 else (fresh, kept)):
-                for b, part in enumerate(parts):
-                    nc.tensor.matmul(turned_acc[:, part], lhsT=term[:, t, cols][:, part], rhs=ident[:], is_transpose=True, start=(i == 0 and b == 0), stop=(i == 1 and b == len(parts) - 1))
-            turned = sb.tile([P, width], F32, name=f"turned{t}_{cols.start}", align_bytes=64)
-            nc.scalar.copy(out=turned[:], in_=turned_acc[:])
-            back_acc = ps.tile([P, width], F32, name=f"back_acc{t}_{cols.start}", tag=f"bank{banks[1]}")
-            for part in parts:
-                nc.tensor.transpose(back_acc[:, part], turned[:, part], ident[:])
-            nc.scalar.copy(out=y[:, t, cols], in_=back_acc[:])
+        def store(t):
+            nc.sync.dma_start(out=out_rows[:, t, :], in_=y[:, t, :])
 
-        add_on_tensor(0, slice(0, S), (0, 1))
-        nc.sync.dma_start(out=out_rows[:, 0, :], in_=y[:, 0, :])
-        add_on_tensor(1, halves[0], (2, 4))
-        add_on_tensor(1, halves[1], (3, 5))
-        nc.sync.dma_start(out=out_rows[:, 1, :], in_=y[:, 1, :])
+        look_up(0, whole)
+        make_fresh(slice(0, 1))
+        make_fresh(slice(1, 2))
+        add(0, whole)
+        store(0)
+        halves = [slice(h * HALF, (h + 1) * HALF) for h in range(2)]
+        nc.scalar.activation(old[:, 0, :], carry_win[1][:].indirect(offs_t[:]), ACT.Copy)
         for cols in halves:
-            look_up(2, cols)
-        for cols in halves:
-            add_on_vector(2, cols)
-        nc.sync.dma_start(out=out_rows[:, 2, :], in_=y[:, 2, :])
+            nc.scalar.activation(old[:, 1, cols], carry_win[2][:].indirect(part_of_offs(cols)), ACT.Copy)
+        make_fresh(slice(2, 4))
+        for t in (1, 2):
+            for cols in halves:
+                nc.vector.tensor_tensor(kept[:, t, cols], old[:, t - 1, cols], keep[:, t, cols], ALU.mult)
+            for cols in halves:
+                add(t, cols)
+            store(t)
         quarters = [slice(h * QUARTER, (h + 1) * QUARTER) for h in range(4)]
-        look_up(last, quarters[0])
-        for h, cols in enumerate(quarters):
-            if h + 1 < len(quarters):
-                look_up(last, quarters[h + 1])
-            add_on_vector(last, cols)
-        nc.sync.dma_start(out=out_rows[:, last, :], in_=y[:, last, :])
+        nc.scalar.activation(old[:, 2, halves[1]], carry_win[last][:].indirect(part_of_offs(halves[1])), ACT.Copy)
+        for cols in quarters[:2]:
+            look_up(last, cols)
+        add(last, quarters[0])
+        nc.vector.tensor_tensor(kept[:, last, halves[1]], old[:, 2, halves[1]], keep[:, last, halves[1]], ALU.mult)
+        add(last, quarters[1])
+        add(last, halves[1])
+        store(last)
 
         y_scales = sb.tile([P, S], U8, name="y_scales", align_bytes=64)
         y_codes = sb.tile([P, S], U32, name="y_codes", align_bytes=64)

@@ -170,21 +170,21 @@ def tile_picked_zgru_mgu_po_kernel(tc, x_words, x_scales, e_words, e_scales, w1,
             nc.sync.dma_start(out=out_rows[:, t, :], in_=y[:, t, :])
 
         look_up(0, whole)
-        make_fresh(slice(0, 1))
-        make_fresh(slice(1, 2))
-        add(0, whole)
-        store(0)
+        make_fresh(slice(0, 2))
         halves = [slice(h * HALF, (h + 1) * HALF) for h in range(2)]
         nc.scalar.activation(old[:, 0, :], carry_win[1][:].indirect(offs_t[:]), ACT.Copy)
         for cols in halves:
             nc.scalar.activation(old[:, 1, cols], carry_win[2][:].indirect(part_of_offs(cols)), ACT.Copy)
         make_fresh(slice(2, 4))
-        for t in (1, 2):
-            for cols in halves:
-                nc.vector.tensor_tensor(kept[:, t, cols], old[:, t - 1, cols], keep[:, t, cols], ALU.mult)
-            for cols in halves:
-                add(t, cols)
+        nc.vector.tensor_tensor(kept[:, 1, :], old[:, 0, :], keep[:, 1, :], ALU.mult)
+        for t in range(2):
+            add(t, whole)
             store(t)
+        for cols in halves:
+            nc.vector.tensor_tensor(kept[:, 2, cols], old[:, 1, cols], keep[:, 2, cols], ALU.mult)
+        for cols in halves:
+            add(2, cols)
+        store(2)
         quarters = [slice(h * QUARTER, (h + 1) * QUARTER) for h in range(4)]
         nc.scalar.activation(old[:, 2, halves[1]], carry_win[last][:].indirect(part_of_offs(halves[1])), ACT.Copy)
         for cols in quarters[:2]:

@@ -48,7 +48,7 @@ def tile_picked_zgru_mgu_po_kernel(tc, x_words, x_scales, e_words, e_scales, w1,
         nc.gpsimd.memset(es_win[:].bitcast(I32), 0)
 
         def load_weight(n, src):
-            raw[n] = sb.tile([P, PACK, N], F32, name="raw_" + n, align_bytes=64)
+            raw[n] = sb.tile([P, PACK, N], F32, name="raw_" + n, tag="raw_" + n, align_bytes=64)
             nc.sync.dma_start(out=raw[n][:], in_=src.rearrange("(p j) c -> p j c", j=PACK))
 
         def load_words(win, src):
@@ -121,17 +121,22 @@ def tile_picked_zgru_mgu_po_kernel(tc, x_words, x_scales, e_words, e_scales, w1,
         nc.vector.tensor_copy(ew[:], e_win[:].bitcast(U32).indirect(tok_t[:]))
         quantise_weight("v1", on_scalar, 1)
         nc.vector.tensor_copy(xw[:], x_win[:].bitcast(U32).indirect(offs_t[:]))
-        keep = sb.tile([P, PACK, S], F32, name="keep", align_bytes=64)
+        keep_first = sb.tile([P, PACK - 1, S], F32, name="keep_first", align_bytes=64)
+        keep = [keep_first[:, t, :] for t in range(PACK - 1)]
         product(z_acc[0], "v1", 0, ew, "e", True)
         for t in range(PACK):
             if t + 1 < PACK:
                 product(z_acc[t + 1], "v1", t + 1, ew, "e", True)
             product(z_acc[t], "w1", t, xw, "x", False)
-            nc.scalar.activation(keep[:, t, :], z_acc[t][:], ACT.Sigmoid, scale=-1.0)
-        quantise_weight("w3", on_vector, 1)
+            if t + 1 < PACK:
+                nc.scalar.activation(keep[t], z_acc[t][:], ACT.Sigmoid, scale=-1.0)
+        quantise_weight("w3", on_vector, 2)
         for t in range(PACK):
             product(g_acc[t], "w3", t, xw, "x", True)
         quantise_weight("v3", (nc.vector.tensor_copy, nc.scalar.copy), 2)
+        keep_last = sb.tile([P, S], F32, name="keep_last", tag="raw_v3", align_bytes=64)
+        keep.append(keep_last[:])
+        nc.scalar.activation(keep[PACK - 1], z_acc[PACK - 1][:], ACT.Sigmoid, scale=-1.0)
 
         y = sb.tile([P, PACK, S], F32, name="y", align_bytes=64)
         out_rows = out_0.rearrange("(p t) c -> p t c", t=PACK)
@@ -158,10 +163,10 @@ def tile_picked_zgru_mgu_po_kernel(tc, x_words, x_scales, e_words, e_scales, w1,
             return offs_t[:, cols.start // GROUP : cols.stop // GROUP]
 
         def look_up(t, cols):
-            nc.vector.tensor_tensor(kept[:, t, cols], carry_win[t][:].indirect(part_of_offs(cols)), keep[:, t, cols], ALU.mult)
+            nc.vector.tensor_tensor(kept[:, t, cols], carry_win[t][:].indirect(part_of_offs(cols)), keep[t][:, cols], ALU.mult)
 
-        def make_fresh(tiles):
-            nc.vector.scalar_tensor_tensor(fresh[:, tiles, :], keep[:, tiles, :], 1.0, cand[:, tiles, :], ALU.subtract, ALU.mult)
+        def make_fresh(tiles, factor):
+            nc.vector.scalar_tensor_tensor(fresh[:, tiles, :], factor, 1.0, cand[:, tiles, :], ALU.subtract, ALU.mult)
 
         def add(t, cols):
             nc.vector.tensor_tensor(y[:, t, cols], kept[:, t, cols], fresh[:, t, cols], ALU.add)
@@ -170,29 +175,35 @@ def tile_picked_zgru_mgu_po_kernel(tc, x_words, x_scales, e_words, e_scales, w1,
             nc.sync.dma_start(out=out_rows[:, t, :], in_=y[:, t, :])
 
         look_up(0, whole)
-        make_fresh(slice(0, 2))
+        make_fresh(slice(0, 2), keep_first[:, 0:2, :])
         halves = [slice(h * HALF, (h + 1) * HALF) for h in range(2)]
         nc.scalar.activation(old[:, 0, :], carry_win[1][:].indirect(offs_t[:]), ACT.Copy)
-        for cols in halves:
+        fetched = [slice(QUARTER, 3 * QUARTER), slice(3 * QUARTER, S)]
+        for cols in fetched:
             nc.scalar.activation(old[:, 1, cols], carry_win[2][:].indirect(part_of_offs(cols)), ACT.Copy)
-        make_fresh(slice(2, 4))
-        nc.vector.tensor_tensor(kept[:, 1, :], old[:, 0, :], keep[:, 1, :], ALU.mult)
-        for t in range(2):
-            add(t, whole)
-            store(t)
-        for cols in halves:
-            nc.vector.tensor_tensor(kept[:, 2, cols], old[:, 1, cols], keep[:, 2, cols], ALU.mult)
+        for t in (2, 3):
+            make_fresh(t, keep[t])
+        add(0, whole)
+        store(0)
+        nc.vector.tensor_tensor(kept[:, 1, :], old[:, 0, :], keep[1], ALU.mult)
+        look_up(2, slice(0, QUARTER))
+        add(1, whole)
+        store(1)
+        for cols in fetched:
+            nc.vector.tensor_tensor(kept[:, 2, cols], old[:, 1, cols], keep[2][:, cols], ALU.mult)
         for cols in halves:
             add(2, cols)
         store(2)
         quarters = [slice(h * QUARTER, (h + 1) * QUARTER) for h in range(4)]
-        nc.scalar.activation(old[:, 2, halves[1]], carry_win[last][:].indirect(part_of_offs(halves[1])), ACT.Copy)
-        for cols in quarters[:2]:
-            look_up(last, cols)
+        middle = slice(QUARTER, SCALAR_COLS)
+        rest = slice(SCALAR_COLS, S)
+        nc.scalar.activation(old[:, 2, rest], carry_win[last][:].indirect(part_of_offs(rest)), ACT.Copy)
+        look_up(last, quarters[0])
+        look_up(last, middle)
         add(last, quarters[0])
-        nc.vector.tensor_tensor(kept[:, last, halves[1]], old[:, 2, halves[1]], keep[:, last, halves[1]], ALU.mult)
-        add(last, quarters[1])
-        add(last, halves[1])
+        nc.vector.tensor_tensor(kept[:, last, rest], old[:, 2, rest], keep[last][:, rest], ALU.mult)
+        add(last, middle)
+        add(last, rest)
         store(last)
 
         y_scales = sb.tile([P, S], U8, name="y_scales", align_bytes=64)

@@ -1,6 +1,7 @@
 from contextlib import ExitStack
 
 import concourse.mybir as mybir
+from concourse.masks import make_identity
 
 K, T, S, W, N = 512, 2048, 512, 1024, 512
 FLOPS = 4 * 2 * K * N * S
@@ -87,6 +88,8 @@ def tile_picked_zgru_mgu_po_kernel(tc, x_words, x_scales, e_words, e_scales, w1,
         xw = sb.tile([P, S], U32, name="xw", align_bytes=64)
         ew = sb.tile([P, S], U32, name="ew", align_bytes=64)
         z_acc = [ps.tile([P, S], F32, name=f"z_acc{t}", tag=f"bank{t}") for t in range(PACK)]
+        ident = sb.tile([P, P], F32, name="ident", align_bytes=64)
+        make_identity(nc, ident[:])
         g_acc = [ps.tile([P, S], F32, name=f"g_acc{t}", tag=f"bank{PACK + t}") for t in range(PACK)]
 
         def product(acc, n, t, words, table, first):
@@ -177,23 +180,36 @@ def tile_picked_zgru_mgu_po_kernel(tc, x_words, x_scales, e_words, e_scales, w1,
         look_up(0, whole)
         make_fresh(slice(0, 2), keep_first[:, 0:2, :])
         halves = [slice(h * HALF, (h + 1) * HALF) for h in range(2)]
-        nc.scalar.activation(old[:, 0, :], carry_win[1][:].indirect(offs_t[:]), ACT.Copy)
-        fetched = [slice(QUARTER, 3 * QUARTER), slice(3 * QUARTER, S)]
-        for cols in fetched:
-            nc.scalar.activation(old[:, 1, cols], carry_win[2][:].indirect(part_of_offs(cols)), ACT.Copy)
+        for cols in halves:
+            nc.scalar.activation(old[:, 0, cols], carry_win[1][:].indirect(part_of_offs(cols)), ACT.Copy)
+        fetched = [(slice(QUARTER, 3 * QUARTER), old[:, 1, :]), (slice(3 * QUARTER, S), y[:, 0, :])]
+        for cols, home in fetched:
+            nc.scalar.activation(home[:, cols], carry_win[2][:].indirect(part_of_offs(cols)), ACT.Copy)
         for t in (2, 3):
             make_fresh(t, keep[t])
-        add(0, whole)
-        store(0)
-        nc.vector.tensor_tensor(kept[:, 1, :], old[:, 0, :], keep[1], ALU.mult)
+        add(0, halves[0])
+        for cols in halves:
+            nc.vector.tensor_tensor(kept[:, 1, cols], old[:, 0, cols], keep[1][:, cols], ALU.mult)
         look_up(2, slice(0, QUARTER))
         add(1, whole)
         store(1)
-        for cols in fetched:
-            nc.vector.tensor_tensor(kept[:, 2, cols], old[:, 1, cols], keep[2][:, cols], ALU.mult)
+        for cols, home in fetched:
+            nc.vector.tensor_tensor(kept[:, 2, cols], home[:, cols], keep[2][:, cols], ALU.mult)
         for cols in halves:
             add(2, cols)
         store(2)
+        blocks = [slice(b, b + P) for b in range(0, HALF, P)]
+        turned_acc = ps.tile([P, HALF], F32, name="turned_acc", tag="bank0")
+        for i, term in enumerate((kept, fresh)):
+            for b, cols in enumerate(blocks):
+                nc.tensor.matmul(turned_acc[:, cols], lhsT=term[:, 0, halves[1]][:, cols], rhs=ident[:], is_transpose=True, start=(i == 0 and b == 0), stop=(i == 1 and b == len(blocks) - 1))
+        turned = sb.tile([P, HALF], F32, name="turned", tag="carry1", align_bytes=64)
+        nc.scalar.copy(out=turned[:], in_=turned_acc[:])
+        back_acc = ps.tile([P, HALF], F32, name="back_acc", tag="bank1")
+        for cols in blocks:
+            nc.tensor.transpose(back_acc[:, cols], turned[:, cols], ident[:])
+        nc.scalar.copy(out=y[:, 0, halves[1]], in_=back_acc[:])
+        store(0)
         quarters = [slice(h * QUARTER, (h + 1) * QUARTER) for h in range(4)]
         middle = slice(QUARTER, SCALAR_COLS)
         rest = slice(SCALAR_COLS, S)

@@ -22,7 +22,8 @@ QUADRANT = 32
 BLOCK_ROWS = 8
 GROUP = 16
 LINE = 4
-SCALAR_COLS = 320
+VECTOR_LOOKS = 320
+SCALAR_COLS = 336
 QUARTER = S // 4
 HALF = S // 2
 
@@ -143,7 +144,10 @@ def tile_picked_zgru_mgu_po_kernel(tc, x_words, x_scales, e_words, e_scales, w1,
 
         y = sb.tile([P, PACK, S], F32, name="y", align_bytes=64)
         out_rows = out_0.rearrange("(p t) c -> p t c", t=PACK)
-        y_bf = sb.tile([P, S * PACK], BF16, name="y_bf", align_bytes=64)
+
+        def round_pair(u, cols):
+            tiles = slice(2 * u, 2 * u + 2)
+            nc.scalar.copy(out=y_bf[:].rearrange("p (c t) -> p c t", t=PACK)[:, cols, tiles], in_=y[:, tiles, cols].rearrange("p t c -> p c t"))
 
         def round_result(copy, c0, c1):
             copy(
@@ -198,6 +202,8 @@ def tile_picked_zgru_mgu_po_kernel(tc, x_words, x_scales, e_words, e_scales, w1,
         for cols in halves:
             add(2, cols)
         store(2)
+        y_bf = sb.tile([P, S * PACK], BF16, name="y_bf", tag="carry2", align_bytes=64)
+        round_pair(0, slice(0, QUARTER))
         blocks = [slice(b, b + P) for b in range(0, HALF, P)]
         turned_acc = ps.tile([P, HALF], F32, name="turned_acc", tag="bank0")
         for i, term in enumerate((kept, fresh)):
@@ -211,8 +217,8 @@ def tile_picked_zgru_mgu_po_kernel(tc, x_words, x_scales, e_words, e_scales, w1,
         nc.scalar.copy(out=y[:, 0, halves[1]], in_=back_acc[:])
         store(0)
         quarters = [slice(h * QUARTER, (h + 1) * QUARTER) for h in range(4)]
-        middle = slice(QUARTER, SCALAR_COLS)
-        rest = slice(SCALAR_COLS, S)
+        middle = slice(QUARTER, VECTOR_LOOKS)
+        rest = slice(VECTOR_LOOKS, S)
         nc.scalar.activation(old[:, 2, rest], carry_win[last][:].indirect(part_of_offs(rest)), ACT.Copy)
         look_up(last, quarters[0])
         look_up(last, middle)
@@ -229,8 +235,8 @@ def tile_picked_zgru_mgu_po_kernel(tc, x_words, x_scales, e_words, e_scales, w1,
         def quantise_result(cols):
             nc.vector.quantize_mx(out=y_codes[:, cols].bitcast(FP8X4), scales=y_scales[:, cols], in_=y_bf[:, cols.start * PACK : cols.stop * PACK])
 
-        for cols in quarters[:2]:
-            round_result(nc.scalar.copy, cols.start, cols.stop)
+        round_pair(1, quarters[0])
+        round_result(nc.scalar.copy, QUARTER, HALF)
         round_result(nc.scalar.copy, HALF, SCALAR_COLS)
         quantise_result(quarters[0])
         round_result(nc.vector.tensor_copy, SCALAR_COLS, S)

@@ -24,6 +24,7 @@ GROUP = 16
 LINE = 4
 VECTOR_LOOKS = 320
 SCALAR_COLS = 336
+ALIGN = 256
 QUARTER = S // 4
 HALF = S // 2
 
@@ -36,21 +37,21 @@ def tile_picked_zgru_mgu_po_kernel(tc, x_words, x_scales, e_words, e_scales, w1,
 
         offs_t = sb.tile([P, S // GROUP], U16, name="offs_t")
         tok_t = sb.tile([P, S // GROUP], U16, name="tok_t")
-        x_win = sb.tile([P, T], I32, name="x_win", align_bytes=64)
-        e_win = sb.tile([P, W], I32, name="e_win", align_bytes=64)
-        xs_win = sb.tile([P, T], U8, name="xs_win", align_bytes=64)
-        es_win = sb.tile([P, W], U8, name="es_win", align_bytes=64)
+        x_win = sb.tile([P, T], I32, name="x_win", align_bytes=ALIGN)
+        e_win = sb.tile([P, W], I32, name="e_win", align_bytes=ALIGN)
+        xs_win = sb.tile([P, T], U8, name="xs_win", align_bytes=ALIGN)
+        es_win = sb.tile([P, W], U8, name="es_win", align_bytes=ALIGN)
         raw = {}
         carry_win = []
-        planes = sb.tile([P, 2 * S], U8, name="planes", align_bytes=64)
-        picked = sb.tile([P, 2 * S], U8, name="picked", align_bytes=64)
+        planes = sb.tile([P, 2 * S], U8, name="planes", align_bytes=ALIGN)
+        picked = sb.tile([P, 2 * S], U8, name="picked", align_bytes=ALIGN)
         plane_cols = {"x": slice(0, S), "e": slice(S, 2 * S)}
 
         nc.vector.memset(xs_win[:].bitcast(I32), 0)
         nc.gpsimd.memset(es_win[:].bitcast(I32), 0)
 
         def load_weight(n, src):
-            raw[n] = sb.tile([P, PACK, N], F32, name="raw_" + n, tag="raw_" + n, align_bytes=64)
+            raw[n] = sb.tile([P, PACK, N], F32, name="raw_" + n, tag="raw_" + n, align_bytes=ALIGN)
             nc.sync.dma_start(out=raw[n][:], in_=src.rearrange("(p j) c -> p j c", j=PACK))
 
         def load_words(win, src):
@@ -75,21 +76,21 @@ def tile_picked_zgru_mgu_po_kernel(tc, x_words, x_scales, e_words, e_scales, w1,
 
         def quantise_weight(n, copies, pieces):
             src = raw[n][:].rearrange("p j (m t) -> p m j t", t=PACK)
-            dealt = sb.tile([P, N * PACK], BF16, name=f"dealt_{n}", align_bytes=64)
+            dealt = sb.tile([P, N * PACK], BF16, name=f"dealt_{n}", align_bytes=ALIGN)
             for u in range(2):
                 pair = dealt[:, u * 2 * N : (u + 1) * 2 * N].rearrange("p (t m j) -> p m j t", t=2, j=PACK)
                 copies[u](out=pair, in_=src[:, :, :, 2 * u : 2 * u + 2])
-            codes[n] = sb.tile([P, N], U32, name=f"codes_{n}", align_bytes=64)
-            scales[n] = sb.tile([P, N], U8, name=f"scales_{n}", align_bytes=64)
+            codes[n] = sb.tile([P, N], U32, name=f"codes_{n}", align_bytes=ALIGN)
+            scales[n] = sb.tile([P, N], U8, name=f"scales_{n}", align_bytes=ALIGN)
             width = N // pieces
             for u in range(pieces):
                 cols = slice(u * width, (u + 1) * width)
                 nc.vector.quantize_mx(out=codes[n][:, cols].bitcast(FP8X4), scales=scales[n][:, cols], in_=dealt[:, u * width * PACK : (u + 1) * width * PACK])
 
-        xw = sb.tile([P, S], U32, name="xw", align_bytes=64)
-        ew = sb.tile([P, S], U32, name="ew", align_bytes=64)
+        xw = sb.tile([P, S], U32, name="xw", align_bytes=ALIGN)
+        ew = sb.tile([P, S], U32, name="ew", align_bytes=ALIGN)
         z_acc = [ps.tile([P, S], F32, name=f"z_acc{t}", tag=f"bank{t}") for t in range(PACK)]
-        ident = sb.tile([P, P], F32, name="ident", align_bytes=64)
+        ident = sb.tile([P, P], F32, name="ident", align_bytes=ALIGN)
         make_identity(nc, ident[:])
         g_acc = [ps.tile([P, S], F32, name=f"g_acc{t}", tag=f"bank{PACK + t}") for t in range(PACK)]
 
@@ -118,14 +119,14 @@ def tile_picked_zgru_mgu_po_kernel(tc, x_words, x_scales, e_words, e_scales, w1,
         load_weight("w3", w3)
         load_weight("v3", v3)
         for t in range(PACK):
-            carry_win.append(sb.tile([P, T], F32, name=f"carry_win{t}", tag=f"carry{t}", align_bytes=64))
+            carry_win.append(sb.tile([P, T], F32, name=f"carry_win{t}", tag=f"carry{t}", align_bytes=ALIGN))
             nc.sync.dma_start(out=carry_win[t][:], in_=carry_rows[t])
 
         quantise_weight("w1", on_scalar, 1)
         nc.vector.tensor_copy(ew[:], e_win[:].bitcast(U32).indirect(tok_t[:]))
         quantise_weight("v1", on_scalar, 1)
         nc.vector.tensor_copy(xw[:], x_win[:].bitcast(U32).indirect(offs_t[:]))
-        keep_first = sb.tile([P, PACK - 1, S], F32, name="keep_first", align_bytes=64)
+        keep_first = sb.tile([P, PACK - 1, S], F32, name="keep_first", align_bytes=ALIGN)
         keep = [keep_first[:, t, :] for t in range(PACK - 1)]
         product(z_acc[0], "v1", 0, ew, "e", True)
         for t in range(PACK):
@@ -138,11 +139,11 @@ def tile_picked_zgru_mgu_po_kernel(tc, x_words, x_scales, e_words, e_scales, w1,
         for t in range(PACK):
             product(g_acc[t], "w3", t, xw, "x", True)
         quantise_weight("v3", (nc.vector.tensor_copy, nc.scalar.copy), 2)
-        keep_last = sb.tile([P, S], F32, name="keep_last", tag="raw_v3", align_bytes=64)
+        keep_last = sb.tile([P, S], F32, name="keep_last", tag="raw_v3", align_bytes=ALIGN)
         keep.append(keep_last[:])
         nc.scalar.activation(keep[PACK - 1], z_acc[PACK - 1][:], ACT.Sigmoid, scale=-1.0)
 
-        y = sb.tile([P, PACK, S], F32, name="y", align_bytes=64)
+        y = sb.tile([P, PACK, S], F32, name="y", align_bytes=ALIGN)
         out_rows = out_0.rearrange("(p t) c -> p t c", t=PACK)
 
         def round_pair(u, cols):
@@ -155,14 +156,14 @@ def tile_picked_zgru_mgu_po_kernel(tc, x_words, x_scales, e_words, e_scales, w1,
                 in_=y[:, :, c0:c1].rearrange("p t (c i) -> p c t i", i=LINE),
             )
 
-        cand = sb.tile([P, PACK, S], F32, name="cand", align_bytes=64)
+        cand = sb.tile([P, PACK, S], F32, name="cand", align_bytes=ALIGN)
         for t in range(PACK):
             product(g_acc[t], "v3", t, ew, "e", False)
             nc.scalar.activation(cand[:, t, :], g_acc[t][:], ACT.Tanh, scale=-1.0)
 
-        fresh = sb.tile([P, PACK, S], F32, name="fresh", align_bytes=64)
-        kept = sb.tile([P, PACK, S], F32, name="kept", align_bytes=64)
-        old = sb.tile([P, 3, S], F32, name="old", align_bytes=64)
+        fresh = sb.tile([P, PACK, S], F32, name="fresh", align_bytes=ALIGN)
+        kept = sb.tile([P, PACK, S], F32, name="kept", align_bytes=ALIGN)
+        old = sb.tile([P, 3, S], F32, name="old", align_bytes=ALIGN)
         last = PACK - 1
         whole = slice(0, S)
 
@@ -202,14 +203,14 @@ def tile_picked_zgru_mgu_po_kernel(tc, x_words, x_scales, e_words, e_scales, w1,
         for cols in halves:
             add(2, cols)
         store(2)
-        y_bf = sb.tile([P, S * PACK], BF16, name="y_bf", tag="carry2", align_bytes=64)
+        y_bf = sb.tile([P, S * PACK], BF16, name="y_bf", tag="carry2", align_bytes=ALIGN)
         round_pair(0, slice(0, QUARTER))
         blocks = [slice(b, b + P) for b in range(0, HALF, P)]
         turned_acc = ps.tile([P, HALF], F32, name="turned_acc", tag="bank0")
         for i, term in enumerate((kept, fresh)):
             for b, cols in enumerate(blocks):
                 nc.tensor.matmul(turned_acc[:, cols], lhsT=term[:, 0, halves[1]][:, cols], rhs=ident[:], is_transpose=True, start=(i == 0 and b == 0), stop=(i == 1 and b == len(blocks) - 1))
-        turned = sb.tile([P, HALF], F32, name="turned", tag="carry1", align_bytes=64)
+        turned = sb.tile([P, HALF], F32, name="turned", tag="carry1", align_bytes=ALIGN)
         nc.scalar.copy(out=turned[:], in_=turned_acc[:])
         back_acc = ps.tile([P, HALF], F32, name="back_acc", tag="bank1")
         for cols in blocks:
@@ -228,8 +229,8 @@ def tile_picked_zgru_mgu_po_kernel(tc, x_words, x_scales, e_words, e_scales, w1,
         add(last, rest)
         store(last)
 
-        y_scales = sb.tile([P, S], U8, name="y_scales", align_bytes=64)
-        y_codes = sb.tile([P, S], U32, name="y_codes", align_bytes=64)
+        y_scales = sb.tile([P, S], U8, name="y_scales", align_bytes=ALIGN)
+        y_codes = sb.tile([P, S], U32, name="y_codes", align_bytes=ALIGN)
         out_words = out_1[0].rearrange("p c r -> p (c r)").bitcast(I32)
 
         def quantise_result(cols):

@@ -192,7 +192,7 @@ def tile_picked_zgru_mgu_po_kernel(tc, x_words, x_scales, e_words, e_scales, w1,
             nc.scalar.activation(home[:, cols], carry_win[2][:].indirect(part_of_offs(cols)), ACT.Copy)
         for t in (2, 3):
             make_fresh(t, keep[t])
-        add(0, halves[0])
+        add(0, slice(0, QUARTER))
         for cols in halves:
             nc.vector.tensor_tensor(kept[:, 1, cols], old[:, 0, cols], keep[1][:, cols], ALU.mult)
         look_up(2, slice(0, QUARTER))
@@ -205,17 +205,19 @@ def tile_picked_zgru_mgu_po_kernel(tc, x_words, x_scales, e_words, e_scales, w1,
         store(2)
         y_bf = sb.tile([P, S * PACK], BF16, name="y_bf", tag="carry2", align_bytes=ALIGN)
         round_pair(0, slice(0, QUARTER))
-        blocks = [slice(b, b + P) for b in range(0, HALF, P)]
-        turned_acc = ps.tile([P, HALF], F32, name="turned_acc", tag="bank0")
+        by_tensor = slice(QUARTER, S)
+        width = S - QUARTER
+        blocks = [slice(b, b + P) for b in range(0, width, P)]
+        turned_acc = ps.tile([P, width], F32, name="turned_acc", tag="bank0")
         for i, term in enumerate((kept, fresh)):
             for b, cols in enumerate(blocks):
-                nc.tensor.matmul(turned_acc[:, cols], lhsT=term[:, 0, halves[1]][:, cols], rhs=ident[:], is_transpose=True, start=(i == 0 and b == 0), stop=(i == 1 and b == len(blocks) - 1))
-        turned = sb.tile([P, HALF], F32, name="turned", tag="carry1", align_bytes=ALIGN)
+                nc.tensor.matmul(turned_acc[:, cols], lhsT=term[:, 0, by_tensor][:, cols], rhs=ident[:], is_transpose=True, start=(i == 0 and b == 0), stop=(i == 1 and b == len(blocks) - 1))
+        turned = sb.tile([P, width], F32, name="turned", tag="carry1", align_bytes=ALIGN)
         nc.scalar.copy(out=turned[:], in_=turned_acc[:])
-        back_acc = ps.tile([P, HALF], F32, name="back_acc", tag="bank1")
+        back_acc = ps.tile([P, width], F32, name="back_acc", tag="bank1")
         for cols in blocks:
             nc.tensor.transpose(back_acc[:, cols], turned[:, cols], ident[:])
-        nc.scalar.copy(out=y[:, 0, halves[1]], in_=back_acc[:])
+        nc.scalar.copy(out=y[:, 0, by_tensor], in_=back_acc[:])
         store(0)
         quarters = [slice(h * QUARTER, (h + 1) * QUARTER) for h in range(4)]
         middle = slice(QUARTER, VECTOR_LOOKS)

@@ -126,22 +126,18 @@ def tile_picked_zgru_mgu_po_kernel(tc, x_words, x_scales, e_words, e_scales, w1,
         nc.vector.tensor_copy(ew[:], e_win[:].bitcast(U32).indirect(tok_t[:]))
         quantise_weight("v1", on_scalar, 1)
         nc.vector.tensor_copy(xw[:], x_win[:].bitcast(U32).indirect(offs_t[:]))
-        keep_first = sb.tile([P, PACK - 1, S], F32, name="keep_first", align_bytes=ALIGN)
-        keep = [keep_first[:, t, :] for t in range(PACK - 1)]
-        product(z_acc[0], "v1", 0, ew, "e", True)
-        for t in range(PACK):
-            if t + 1 < PACK:
-                product(z_acc[t + 1], "v1", t + 1, ew, "e", True)
-            product(z_acc[t], "w1", t, xw, "x", False)
-            if t + 1 < PACK:
+        keep_all = sb.tile([P, PACK, S], F32, name="keep_all", align_bytes=ALIGN)
+        keep = [keep_all[:, t, :] for t in range(PACK)]
+        for pair in ((0, 1), (2,), (3,)):
+            for t in pair:
+                product(z_acc[t], "v1", t, ew, "e", True)
+            for t in pair:
+                product(z_acc[t], "w1", t, xw, "x", False)
                 nc.scalar.activation(keep[t], z_acc[t][:], ACT.Sigmoid, scale=-1.0)
         quantise_weight("w3", on_vector, 2)
         for t in range(PACK):
             product(g_acc[t], "w3", t, xw, "x", True)
         quantise_weight("v3", (nc.vector.tensor_copy, nc.scalar.copy), 2)
-        keep_last = sb.tile([P, S], F32, name="keep_last", tag="raw_v3", align_bytes=ALIGN)
-        keep.append(keep_last[:])
-        nc.scalar.activation(keep[PACK - 1], z_acc[PACK - 1][:], ACT.Sigmoid, scale=-1.0)
 
         y = sb.tile([P, PACK, S], F32, name="y", align_bytes=ALIGN)
         out_rows = out_0.rearrange("(p t) c -> p t c", t=PACK)
@@ -183,15 +179,14 @@ def tile_picked_zgru_mgu_po_kernel(tc, x_words, x_scales, e_words, e_scales, w1,
             nc.sync.dma_start(out=out_rows[:, t, :], in_=y[:, t, :])
 
         look_up(0, whole)
-        make_fresh(slice(0, 2), keep_first[:, 0:2, :])
+        make_fresh(slice(0, 2), keep_all[:, 0:2, :])
         halves = [slice(h * HALF, (h + 1) * HALF) for h in range(2)]
         for cols in halves:
             nc.scalar.activation(old[:, 0, cols], carry_win[1][:].indirect(part_of_offs(cols)), ACT.Copy)
         fetched = [(slice(QUARTER, 3 * QUARTER), old[:, 1, :]), (slice(3 * QUARTER, S), y[:, 0, :])]
         for cols, home in fetched:
             nc.scalar.activation(home[:, cols], carry_win[2][:].indirect(part_of_offs(cols)), ACT.Copy)
-        for t in (2, 3):
-            make_fresh(t, keep[t])
+        make_fresh(slice(2, 4), keep_all[:, 2:4, :])
         add(0, slice(0, QUARTER))
         for cols in halves:
             nc.vector.tensor_tensor(kept[:, 1, cols], old[:, 0, cols], keep[1][:, cols], ALU.mult)

@@ -24,7 +24,7 @@ GROUP = 16
 LINE = 4
 VECTOR_LOOKS = 320
 SCALAR_COLS = 336
-ALIGN = 256
+ALIGN = 1024
 QUARTER = S // 4
 HALF = S // 2
 

from contextlib import ExitStack

import concourse.mybir as mybir
from concourse.masks import make_identity

K, T, S, W, N = 512, 2048, 512, 1024, 512
FLOPS = 4 * 2 * K * N * S

F32 = mybir.dt.float32
BF16 = mybir.dt.bfloat16
I32 = mybir.dt.int32
U32 = mybir.dt.uint32
U16 = mybir.dt.uint16
U8 = mybir.dt.uint8
FP8X4 = mybir.dt.float8_e4m3fn_x4
ALU = mybir.AluOpType
ACT = mybir.ActivationFunctionType

P = 128
PACK = 4
QUADRANT = 32
BLOCK_ROWS = 8
GROUP = 16
LINE = 4
VECTOR_LOOKS = 320
SCALAR_COLS = 336
ALIGN = 1024
QUARTER = S // 4
HALF = S // 2


def tile_picked_zgru_mgu_po_kernel(tc, x_words, x_scales, e_words, e_scales, w1, v1, w3, v3, carry, offs, tok, out_0, out_1, out_2):
    nc = tc.nc
    with ExitStack() as ctx:
        sb = ctx.enter_context(tc.tile_pool(name="sb", bufs=1))
        ps = ctx.enter_context(tc.psum_pool(name="ps", bufs=1))

        offs_t = sb.tile([P, S // GROUP], U16, name="offs_t")
        tok_t = sb.tile([P, S // GROUP], U16, name="tok_t")
        x_win = sb.tile([P, T], I32, name="x_win", align_bytes=ALIGN)
        e_win = sb.tile([P, W], I32, name="e_win", align_bytes=ALIGN)
        xs_win = sb.tile([P, T], U8, name="xs_win", align_bytes=ALIGN)
        es_win = sb.tile([P, W], U8, name="es_win", align_bytes=ALIGN)
        raw = {}
        carry_win = []
        planes = sb.tile([P, 2 * S], U8, name="planes", align_bytes=ALIGN)
        picked = sb.tile([P, 2 * S], U8, name="picked", align_bytes=ALIGN)
        plane_cols = {"x": slice(0, S), "e": slice(S, 2 * S)}

        nc.vector.memset(xs_win[:].bitcast(I32), 0)
        nc.gpsimd.memset(es_win[:].bitcast(I32), 0)

        def load_weight(n, src):
            raw[n] = sb.tile([P, PACK, N], F32, name="raw_" + n, tag="raw_" + n, align_bytes=ALIGN)
            nc.sync.dma_start(out=raw[n][:], in_=src.rearrange("(p j) c -> p j c", j=PACK))

        def load_words(win, src):
            nc.sync.dma_start(out=win[:], in_=src[0].rearrange("p c r -> p (c r)").bitcast(I32))

        def load_scale_rows(win, src):
            nc.sync.dma_start(out=win[0:P:BLOCK_ROWS, :].bitcast(I32), in_=src[0].bitcast(I32))

        carry_rows = carry.rearrange("(p t) c -> t p c", t=PACK)

        load_weight("w1", w1)
        nc.sync.dma_start(offs_t[:], offs)
        nc.sync.dma_start(tok_t[:], tok)
        load_scale_rows(xs_win, x_scales)
        load_scale_rows(es_win, e_scales)
        load_weight("v1", v1)
        load_words(e_win, e_words)
        load_words(x_win, x_words)

        codes = {}
        scales = {}

        def quantise_weight(n, copies, pieces):
            src = raw[n][:].rearrange("p j (m t) -> p m j t", t=PACK)
            dealt = sb.tile([P, N * PACK], BF16, name=f"dealt_{n}", align_bytes=ALIGN)
            for u in range(2):
                pair = dealt[:, u * 2 * N : (u + 1) * 2 * N].rearrange("p (t m j) -> p m j t", t=2, j=PACK)
                copies[u](out=pair, in_=src[:, :, :, 2 * u : 2 * u + 2])
            codes[n] = sb.tile([P, N], U32, name=f"codes_{n}", align_bytes=ALIGN)
            scales[n] = sb.tile([P, N], U8, name=f"scales_{n}", align_bytes=ALIGN)
            width = N // pieces
            for u in range(pieces):
                cols = slice(u * width, (u + 1) * width)
                nc.vector.quantize_mx(out=codes[n][:, cols].bitcast(FP8X4), scales=scales[n][:, cols], in_=dealt[:, u * width * PACK : (u + 1) * width * PACK])

        xw = sb.tile([P, S], U32, name="xw", align_bytes=ALIGN)
        ew = sb.tile([P, S], U32, name="ew", align_bytes=ALIGN)
        z_acc = [ps.tile([P, S], F32, name=f"z_acc{t}", tag=f"bank{t}") for t in range(PACK)]
        ident = sb.tile([P, P], F32, name="ident", align_bytes=ALIGN)
        make_identity(nc, ident[:])
        g_acc = [ps.tile([P, S], F32, name=f"g_acc{t}", tag=f"bank{PACK + t}") for t in range(PACK)]

        def product(acc, n, t, words, table, first):
            cols = slice(t * P, (t + 1) * P)
            nc.tensor.matmul_mx(
                out=acc[:],
                lhsT=codes[n][:, cols].bitcast(FP8X4),
                lhsT_scale=scales[n][:, cols],
                rhs=words[:].bitcast(FP8X4),
                rhs_scale=planes[:, plane_cols[table]],
                start=first,
                stop=not first,
            )

        on_vector = (nc.vector.tensor_copy, nc.vector.tensor_copy)
        on_scalar = (nc.scalar.copy, nc.scalar.copy)
        nc.vector.tensor_copy(picked[:, plane_cols["x"]], xs_win[:].indirect(offs_t[:]))
        nc.vector.tensor_copy(picked[:, plane_cols["e"]], es_win[:].indirect(tok_t[:]))
        nc.vector.tensor_copy(planes[:].bitcast(I32), picked[:].bitcast(I32))
        for r in range(1, 4):
            nc.sync.dma_start(
                out=planes[r:P:QUADRANT, :].bitcast(I32),
                in_=picked[BLOCK_ROWS * r : P : QUADRANT, :].bitcast(I32),
            )
        load_weight("w3", w3)
        load_weight("v3", v3)
        for t in range(PACK):
            carry_win.append(sb.tile([P, T], F32, name=f"carry_win{t}", tag=f"carry{t}", align_bytes=ALIGN))
            nc.sync.dma_start(out=carry_win[t][:], in_=carry_rows[t])

        quantise_weight("w1", on_scalar, 1)
        nc.vector.tensor_copy(ew[:], e_win[:].bitcast(U32).indirect(tok_t[:]))
        quantise_weight("v1", on_scalar, 1)
        nc.vector.tensor_copy(xw[:], x_win[:].bitcast(U32).indirect(offs_t[:]))
        keep_all = sb.tile([P, PACK, S], F32, name="keep_all", align_bytes=ALIGN)
        keep = [keep_all[:, t, :] for t in range(PACK)]
        for pair in ((0, 1), (2,), (3,)):
            for t in pair:
                product(z_acc[t], "v1", t, ew, "e", True)
            for t in pair:
                product(z_acc[t], "w1", t, xw, "x", False)
                nc.scalar.activation(keep[t], z_acc[t][:], ACT.Sigmoid, scale=-1.0)
        quantise_weight("w3", on_vector, 2)
        for t in range(PACK):
            product(g_acc[t], "w3", t, xw, "x", True)
        quantise_weight("v3", (nc.vector.tensor_copy, nc.scalar.copy), 2)

        y = sb.tile([P, PACK, S], F32, name="y", align_bytes=ALIGN)
        out_rows = out_0.rearrange("(p t) c -> p t c", t=PACK)

        def round_pair(u, cols):
            tiles = slice(2 * u, 2 * u + 2)
            nc.scalar.copy(out=y_bf[:].rearrange("p (c t) -> p c t", t=PACK)[:, cols, tiles], in_=y[:, tiles, cols].rearrange("p t c -> p c t"))

        def round_result(copy, c0, c1):
            copy(
                out=y_bf[:, c0 * PACK : c1 * PACK].rearrange("p (c i t) -> p c t i", i=LINE, t=PACK),
                in_=y[:, :, c0:c1].rearrange("p t (c i) -> p c t i", i=LINE),
            )

        cand = sb.tile([P, PACK, S], F32, name="cand", align_bytes=ALIGN)
        for t in range(PACK):
            product(g_acc[t], "v3", t, ew, "e", False)
            nc.scalar.activation(cand[:, t, :], g_acc[t][:], ACT.Tanh, scale=-1.0)

        fresh = sb.tile([P, PACK, S], F32, name="fresh", align_bytes=ALIGN)
        kept = sb.tile([P, PACK, S], F32, name="kept", align_bytes=ALIGN)
        old = sb.tile([P, 3, S], F32, name="old", align_bytes=ALIGN)
        last = PACK - 1
        whole = slice(0, S)

        def part_of_offs(cols):
            return offs_t[:, cols.start // GROUP : cols.stop // GROUP]

        def look_up(t, cols):
            nc.vector.tensor_tensor(kept[:, t, cols], carry_win[t][:].indirect(part_of_offs(cols)), keep[t][:, cols], ALU.mult)

        def make_fresh(tiles, factor):
            nc.vector.scalar_tensor_tensor(fresh[:, tiles, :], factor, 1.0, cand[:, tiles, :], ALU.subtract, ALU.mult)

        def add(t, cols):
            nc.vector.tensor_tensor(y[:, t, cols], kept[:, t, cols], fresh[:, t, cols], ALU.add)

        def store(t):
            nc.sync.dma_start(out=out_rows[:, t, :], in_=y[:, t, :])

        look_up(0, whole)
        make_fresh(slice(0, 2), keep_all[:, 0:2, :])
        halves = [slice(h * HALF, (h + 1) * HALF) for h in range(2)]
        for cols in halves:
            nc.scalar.activation(old[:, 0, cols], carry_win[1][:].indirect(part_of_offs(cols)), ACT.Copy)
        fetched = [(slice(QUARTER, 3 * QUARTER), old[:, 1, :]), (slice(3 * QUARTER, S), y[:, 0, :])]
        for cols, home in fetched:
            nc.scalar.activation(home[:, cols], carry_win[2][:].indirect(part_of_offs(cols)), ACT.Copy)
        make_fresh(slice(2, 4), keep_all[:, 2:4, :])
        add(0, slice(0, QUARTER))
        for cols in halves:
            nc.vector.tensor_tensor(kept[:, 1, cols], old[:, 0, cols], keep[1][:, cols], ALU.mult)
        look_up(2, slice(0, QUARTER))
        add(1, whole)
        store(1)
        for cols, home in fetched:
            nc.vector.tensor_tensor(kept[:, 2, cols], home[:, cols], keep[2][:, cols], ALU.mult)
        for cols in halves:
            add(2, cols)
        store(2)
        y_bf = sb.tile([P, S * PACK], BF16, name="y_bf", tag="carry2", align_bytes=ALIGN)
        round_pair(0, slice(0, QUARTER))
        by_tensor = slice(QUARTER, S)
        width = S - QUARTER
        blocks = [slice(b, b + P) for b in range(0, width, P)]
        turned_acc = ps.tile([P, width], F32, name="turned_acc", tag="bank0")
        for i, term in enumerate((kept, fresh)):
            for b, cols in enumerate(blocks):
                nc.tensor.matmul(turned_acc[:, cols], lhsT=term[:, 0, by_tensor][:, cols], rhs=ident[:], is_transpose=True, start=(i == 0 and b == 0), stop=(i == 1 and b == len(blocks) - 1))
        turned = sb.tile([P, width], F32, name="turned", tag="carry1", align_bytes=ALIGN)
        nc.scalar.copy(out=turned[:], in_=turned_acc[:])
        back_acc = ps.tile([P, width], F32, name="back_acc", tag="bank1")
        for cols in blocks:
            nc.tensor.transpose(back_acc[:, cols], turned[:, cols], ident[:])
        nc.scalar.copy(out=y[:, 0, by_tensor], in_=back_acc[:])
        store(0)
        quarters = [slice(h * QUARTER, (h + 1) * QUARTER) for h in range(4)]
        middle = slice(QUARTER, VECTOR_LOOKS)
        rest = slice(VECTOR_LOOKS, S)
        nc.scalar.activation(old[:, 2, rest], carry_win[last][:].indirect(part_of_offs(rest)), ACT.Copy)
        look_up(last, quarters[0])
        look_up(last, middle)
        add(last, quarters[0])
        nc.vector.tensor_tensor(kept[:, last, rest], old[:, 2, rest], keep[last][:, rest], ALU.mult)
        add(last, middle)
        add(last, rest)
        store(last)

        y_scales = sb.tile([P, S], U8, name="y_scales", align_bytes=ALIGN)
        y_codes = sb.tile([P, S], U32, name="y_codes", align_bytes=ALIGN)
        out_words = out_1[0].rearrange("p c r -> p (c r)").bitcast(I32)

        def quantise_result(cols):
            nc.vector.quantize_mx(out=y_codes[:, cols].bitcast(FP8X4), scales=y_scales[:, cols], in_=y_bf[:, cols.start * PACK : cols.stop * PACK])

        round_pair(1, quarters[0])
        round_result(nc.scalar.copy, QUARTER, HALF)
        round_result(nc.scalar.copy, HALF, SCALAR_COLS)
        quantise_result(quarters[0])
        round_result(nc.vector.tensor_copy, SCALAR_COLS, S)
        quantise_result(quarters[1])
        quantise_result(halves[1])
        for cols in halves:
            nc.sync.dma_start(out=out_words[:, cols], in_=y_codes[:, cols].bitcast(I32))
        for q, queue in enumerate((nc.sync, nc.sync, nc.scalar, nc.scalar)):
            queue.dma_start(
                out=out_2[0, 4 * q : 4 * q + 4, :].bitcast(I32),
                in_=y_scales[QUADRANT * q : QUADRANT * q + 4, :].bitcast(I32),
            )
